import numpy as np
import ml_dtypes


def mxq(x, axis, fmt="e4m3"):
    dtype, down = {"e4m3": (ml_dtypes.float8_e4m3fn, 7), "e5m2": (ml_dtypes.float8_e5m2, 14)}[fmt]
    v = np.moveaxis(np.asarray(x, np.float32).astype(ml_dtypes.bfloat16).astype(np.float64), axis, -1)
    blocks = v.reshape(v.shape[:-1] + (-1, 32))
    amax = np.abs(blocks).max(-1, keepdims=True)
    byte = np.maximum(np.where(amax > 0, np.frexp(amax)[1] - 1 + 127, 0) - down, 1)
    scale = np.exp2(byte - 127.0)
    codes = (blocks / scale).astype(np.float32).astype(dtype).astype(np.float64)
    return np.moveaxis((codes * scale).reshape(v.shape), -1, axis)


WIDE = False


def mx_kscale(k):
    if not WIDE:
        return np.ones(k)
    levels = np.array([10, -10, 5, -5, 0])
    if k % 512:
        return np.exp2(np.random.permutation(np.resize(levels, k // 32))).repeat(32)
    a = np.empty((k // 512, 16))
    for p in range(k // 512):
        a[p, :8] = np.random.permutation(np.resize(levels, 8))
        for g in range(8):
            far = levels[np.abs(levels - a[p, g]) >= 10]
            a[p, g + 8] = far[np.random.randint(len(far))]
    return np.exp2(a.ravel()).repeat(32)


BF16 = ml_dtypes.bfloat16


def bf(x):
    return np.asarray(x, np.float32).astype(BF16)


def f64(x):
    return np.asarray(x).astype(np.float64)


B, P, S, K, C = 4, 2048, 1024, 512, 128


def instance_norm(x):
    mu = np.mean(x, axis=1, keepdims=True)
    centered = x - mu
    var = np.mean(centered * centered, axis=1, keepdims=True)
    return centered / np.sqrt(var + 1e-5)


def draw0():
    s, t = mx_kscale(S), mx_kscale(K)
    return {
        "x": bf(0.5 + 1.5 * np.random.standard_normal((B, P, C))),
        "m": bf(np.random.standard_normal((B, P, S)) * s),
        "wm": bf(np.random.standard_normal((S, K)) / np.sqrt(S) / s[:, None]),
        "bm": bf(0.3 * np.random.standard_normal(K)),
        "g": bf(np.random.standard_normal(K) * t),
        "wg": bf(np.random.standard_normal((K, C)) / np.sqrt(K) / t[:, None]),
        "wb": bf(np.random.standard_normal((K, C)) / np.sqrt(K) / t[:, None]),
    }


def core(x, m, wm, bm, g, wg, wb):
    h = (mxq(f64(m), 2, "e4m3") @ mxq(f64(wm), 0, "e4m3")) + f64(bm)[None, None, :]
    a = np.maximum(h, 0.0) * f64(g)[None, None, :]
    aq = mxq(a, 2, "e4m3")
    gamma = aq @ mxq(f64(wg), 0, "e4m3")
    beta = aq @ mxq(f64(wb), 0, "e4m3")
    xn = instance_norm(f64(x))
    y = xn * (1.0 + gamma) + beta
    return np.where(y >= 0.0, y, 0.2 * y)


def e4m3fn_bytes(y):
    return np.clip(np.asarray(y, np.float64), -448.0, 448.0).astype(np.float32).astype(ml_dtypes.float8_e4m3fn).view(np.uint8)


def e4m3fn_values(b):
    return np.asarray(b, np.uint8).view(ml_dtypes.float8_e4m3fn).astype(np.float64)


def setup_inputs():
    d = draw0()
    x0 = np.asarray(d['m']).astype(np.float64)
    s = (np.max(np.abs(x0), axis=(0, 1), keepdims=True) / 448.0).astype(np.float32)
    out = {}
    for k, v in d.items():
        if k == 'm':
            out['m_bytes'] = e4m3fn_bytes(x0 / s.astype(np.float64))
            out['m_scale'] = s
        else:
            out[k] = v
    return out


def reference(x, m_bytes, m_scale, wm, bm, g, wg, wb):
    return core(x, e4m3fn_values(m_bytes) * m_scale.astype(np.float64), wm, bm, g, wg, wb)

@@ -1,0 +1,323 @@
+from contextlib import ExitStack
+
+import concourse.mybir as mybir
+from concourse.masks import make_identity
+
+B, POS, S, K, C = 4, 2048, 1024, 512, 128
+FLOPS = 2 * B * POS * (S * K + 2 * K * C)
+
+F32 = mybir.dt.float32
+BF16 = mybir.dt.bfloat16
+U32 = mybir.dt.uint32
+U8 = mybir.dt.uint8
+FP8 = mybir.dt.float8_e4m3fn
+X4 = mybir.dt.float8_e4m3fn_x4
+ALU = mybir.AluOpType
+ACT = mybir.ActivationFunctionType
+
+P = 128
+ROWS = POS // P
+CR = 4
+NT = CR * P
+CPS = ROWS // CR
+NCH = B * CPS
+G = S // 512
+
+
+def tile_spademodulationpointwise_t_kernel(tc, x, m_bytes, m_scale, wm, bm, g, wg, wb, out):
+    nc = tc.nc
+    with ExitStack() as ctx:
+        keep = ctx.enter_context(tc.tile_pool(name="keep", bufs=1))
+        pool = ctx.enter_context(tc.tile_pool(name="pool", bufs=2))
+        psum = ctx.enter_context(tc.psum_pool(name="psum", bufs=1))
+        ctx.enter_context(tc.manual_schedule())
+
+        m_view = m_bytes.rearrange("b (p i) k -> b p (i k)", i=ROWS)
+        x_view = x.rearrange("b (p i) c -> b p i c", i=ROWS)
+        out_view = out.rearrange("b (p i) c -> b p i c", i=ROWS)
+        wm_view = wm.rearrange("(g p j) c -> g p (j c)", p=P, j=4)
+
+        codes_in = [keep.tile([P, CR * S], U8, name=f"codes_in{c}", align_bytes=64) for c in range(NCH)]
+        x_sb = [keep.tile([P, ROWS, C], BF16, name=f"x_sb{b}", align_bytes=64) for b in range(B)]
+        wm_raw = [keep.tile([P, 4 * K], BF16, name=f"wm_raw{i}", align_bytes=64) for i in range(G)]
+        w2_raw = keep.tile([P, 2, 4, C], BF16, name="w2_raw", align_bytes=64)
+        scale4 = keep.tile([P, G, 4], F32, name="scale4")
+        gain_raw = keep.tile([P, 4], BF16, name="gain_raw")
+        bias_raw = keep.tile([P, 4], BF16, name="bias_raw")
+
+        def load_codes(c, i0, i1):
+            b, j = divmod(c, CPS)
+            nc.sync.dma_start(
+                out=codes_in[c][:, i0 * S : i1 * S],
+                in_=m_view[b][:, (j * CR + i0) * S : (j * CR + i1) * S],
+            )
+
+        load_codes(0, 0, 1)
+        load_codes(0, 1, 2)
+        nc.scalar.dma_start(out=scale4[:], in_=m_scale.rearrange("a b (g p t) -> p g (a b t)", g=G, t=4))
+        nc.scalar.dma_start(out=gain_raw[:], in_=g.rearrange("(p t) -> p t", t=4))
+        nc.scalar.dma_start(out=bias_raw[:], in_=bm.rearrange("(p t) -> p t", t=4))
+        nc.sync.dma_start(out=wm_raw[0][:], in_=wm_view[0])
+        load_codes(0, 2, 4)
+        nc.sync.dma_start(out=wm_raw[1][:], in_=wm_view[1])
+        load_codes(1, 0, 4)
+        nc.sync.dma_start(out=w2_raw[:, 0], in_=wg.rearrange("(p j) c -> p j c", j=4))
+        nc.sync.dma_start(out=w2_raw[:, 1], in_=wb.rearrange("(p j) c -> p j c", j=4))
+        nc.sync.dma_start(out=x_sb[0][:], in_=x_view[0])
+        for c in range(2, NCH):
+            load_codes(c, 0, 4)
+            if c % CPS == 1 and c > 1:
+                nc.sync.dma_start(out=x_sb[c // CPS][:], in_=x_view[c // CPS])
+
+        warm = keep.tile([P, 1], F32, name="warm")
+        nc.vector.memset(warm[:], 1.0)
+        nc.scalar.activation(out=warm[:], in_=warm[:], func=ACT.Sqrt)
+        ident_f = keep.tile([P, P], F32, name="ident_f")
+        make_identity(nc, ident_f[:])
+        ident_b = keep.tile([P, P], BF16, name="ident_b")
+        nc.vector.tensor_copy(out=ident_b[:], in_=ident_f[:])
+        sign4 = keep.tile([P, 4], F32, name="sign4")
+        gain4 = keep.tile([P, 4], F32, name="gain4")
+        bias4 = keep.tile([P, 4], F32, name="bias4")
+        nc.scalar.activation(out=sign4[:], in_=gain_raw[:], func=ACT.Sign)
+        nc.scalar.activation(out=gain4[:], in_=gain_raw[:], func=ACT.Abs)
+        nc.vector.tensor_tensor(out=bias4[:], in0=bias_raw[:], in1=gain4[:], op=ALU.mult)
+
+        wm_codes = [keep.tile([P, K], U32, name=f"wm_codes{i}", align_bytes=64) for i in range(G)]
+        wm_scales = [keep.tile([P, K], U8, name=f"wm_scales{i}", align_bytes=64) for i in range(G)]
+        wm_grp = [keep.tile([P, 4 * K], BF16, name=f"wm_grp{i}", align_bytes=64) for i in range(G)]
+        w2_codes = keep.tile([P, 2 * C], U32, name="w2_codes", align_bytes=64)
+        w2_scales = keep.tile([P, 2 * C], U8, name="w2_scales", align_bytes=64)
+        w2_grp = keep.tile([P, 2, C, 4], BF16, name="w2_grp", align_bytes=64)
+
+        def group_wm(i, eng):
+            src = wm_raw[i][:].rearrange("p (j m t) -> p t m j", j=4, t=4)
+            dst = wm_grp[i][:].rearrange("p (t m j) -> p t m j", t=4, j=4)
+            for t in range(4):
+                if eng == "v":
+                    nc.vector.tensor_copy(out=dst[:, t], in_=src[:, t])
+                else:
+                    nc.gpsimd.tensor_scalar(out=dst[:, t], in0=src[:, t], scalar1=1.0, scalar2=0.0, op0=ALU.mult, op1=ALU.add)
+
+        def quantise_wm(i):
+            nc.vector.quantize_mx(out=wm_codes[i][:].bitcast(X4), scales=wm_scales[i][:], in_=wm_grp[i][:])
+
+        def group_w2(w):
+            nc.vector.tensor_tensor(
+                out=w2_grp[:, w],
+                in0=w2_raw[:, w].rearrange("p j c -> p c j"),
+                in1=sign4[:].unsqueeze(1).to_broadcast([P, C, 4]),
+                op=ALU.mult,
+            )
+
+        def quantise_w2():
+            nc.vector.quantize_mx(
+                out=w2_codes[:].bitcast(X4), scales=w2_scales[:], in_=w2_grp[:].rearrange("p w c j -> p (w c j)")
+            )
+
+        wide, mgrp, mq, hp, apl, agrp, aq, gb, xn, stat, mur, ep = {}, {}, {}, {}, {}, {}, {}, {}, {}, {}, {}, {}
+
+        def widen(c, i):
+            if i == 0:
+                wide[c] = pool.tile([P, CR * S], BF16, name="wide", align_bytes=64, bufs=2)
+            cols = slice(i * S, (i + 1) * S)
+            if c == 0 and i % 2 == 1:
+                nc.vector.tensor_copy(out=wide[c][:, cols], in_=codes_in[c][:, cols].bitcast(FP8))
+            else:
+                nc.scalar.copy(out=wide[c][:, cols], in_=codes_in[c][:, cols].bitcast(FP8))
+
+        def turn(c, k):
+            gg, h = divmod(k, 2)
+            words = wide[c][:].bitcast(F32)
+            bank = psum.tile([P, 2, 256], F32, name="turned", bufs=3)
+            for i2 in range(2):
+                i = 2 * h + i2
+                for u in range(2):
+                    lo = i * (S // 2) + 256 * gg + u
+                    nc.tensor.transpose(bank[:, u, i2 * P : (i2 + 1) * P], words[:, lo : lo + 255 : 2], ident_f[:])
+            ep[("bank", c, k)] = bank
+
+        def scale_up(c, k):
+            gg, h = divmod(k, 2)
+            if k == 0:
+                mgrp[c] = pool.tile([P, G, NT * 4], BF16, name="mgrp", align_bytes=64, bufs=2)
+            bank = ep.pop(("bank", c, k))
+            src = bank[:].rearrange("p u r -> p (u r)").bitcast(BF16).rearrange("p (u r e) -> p r u e", u=2, e=2)
+            dst = mgrp[c][:, gg, h * 1024 : (h + 1) * 1024].rearrange("p (r u e) -> p r u e", u=2, e=2)
+            sc = scale4[:, gg].rearrange("p (u e) -> p u e", e=2).unsqueeze(1).to_broadcast([P, 256, 2, 2])
+            nc.vector.tensor_tensor(out=dst, in0=src, in1=sc, op=ALU.mult)
+
+        def quantise_m(c):
+            codes = pool.tile([P, G * NT], U32, name="m_codes", align_bytes=64, bufs=2)
+            scales = pool.tile([P, G * NT], U8, name="m_scales", align_bytes=64, bufs=2)
+            nc.vector.quantize_mx(
+                out=codes[:].bitcast(X4), scales=scales[:], in_=mgrp.pop(c)[:].rearrange("p g n -> p (g n)")
+            )
+            mq[c] = (codes, scales)
+
+        def embed(c, t):
+            h = psum.tile([P, NT], F32, name="embed", bufs=3)
+            for gg in range(G):
+                codes, scales = mq[c]
+                tok = slice(gg * NT, (gg + 1) * NT)
+                cols = slice(t * P, (t + 1) * P)
+                nc.tensor.matmul_mx(
+                    out=h[:],
+                    lhsT=wm_codes[gg][:, cols].bitcast(X4),
+                    lhsT_scale=wm_scales[gg][:, cols],
+                    rhs=codes[:, tok].bitcast(X4),
+                    rhs_scale=scales[:, tok],
+                    start=(gg == 0),
+                    stop=(gg == G - 1),
+                )
+            hp[(c, t)] = h
+
+        def rectify(c, t):
+            if t == 0:
+                apl[c] = pool.tile([P, 4, NT], BF16, name="apl", align_bytes=64, bufs=2)
+            nc.scalar.activation(
+                out=apl[c][:, t], in_=hp.pop((c, t))[:], func=ACT.Relu, bias=bias4[:, t : t + 1], scale=gain4[:, t : t + 1]
+            )
+
+        def interleave(c):
+            agrp[c] = pool.tile([P, NT, 4], BF16, name="agrp", align_bytes=64, bufs=2)
+            src = apl.pop(c)[:].rearrange("p t n -> p n t")
+            if c == NCH - 1:
+                nc.vector.tensor_copy(out=agrp[c][:], in_=src)
+            else:
+                nc.gpsimd.tensor_scalar(out=agrp[c][:], in0=src, scalar1=1.0, scalar2=0.0, op0=ALU.mult, op1=ALU.add)
+
+        def quantise_a(c):
+            codes = pool.tile([P, NT], U32, name="a_codes", align_bytes=64, bufs=2)
+            scales = pool.tile([P, NT], U8, name="a_scales", align_bytes=64, bufs=2)
+            nc.vector.quantize_mx(
+                out=codes[:].bitcast(X4), scales=scales[:], in_=agrp.pop(c)[:].rearrange("p n t -> p (n t)")
+            )
+            aq[c] = (codes, scales)
+
+        def maps(c):
+            codes, scales = aq.pop(c)
+            gam = psum.tile([P, CR, C], F32, name="gam", bufs=1)
+            bet = psum.tile([P, CR, C], F32, name="bet", bufs=1)
+            for i in range(CR):
+                cols = slice(i * P, (i + 1) * P)
+                for w, dst in ((0, gam), (1, bet)):
+                    wc = slice(w * C, (w + 1) * C)
+                    nc.tensor.matmul_mx(
+                        out=dst[:, i],
+                        lhsT=codes[:, cols].bitcast(X4),
+                        lhsT_scale=scales[:, cols],
+                        rhs=w2_codes[:, wc].bitcast(X4),
+                        rhs_scale=w2_scales[:, wc],
+                        start=True,
+                        stop=True,
+                    )
+            gb[c] = (gam, bet)
+
+        def stats_turn(b, h):
+            if h == 0:
+                stat[b] = keep.tile([P, 4, 6], F32, name=f"bnst{b}")
+            bank = psum.tile([P, 8, P], BF16, name="turned", bufs=3)
+            for i in range(8):
+                nc.tensor.transpose(bank[:, i], x_sb[b][:, h * 8 + i], ident_b[:])
+            for q in range(2):
+                nc.vector.bn_stats(out=stat[b][:, 2 * h + q], in_=bank[:, 4 * q : 4 * q + 4].rearrange("p i c -> p (i c)"))
+
+        def stats_aggr(b):
+            mv = keep.tile([P, 2], F32, name=f"mv{b}")
+            nc.vector.bn_aggr(out=mv[:], in_=stat[b][:].rearrange("p a s -> p (a s)"))
+            sd = keep.tile([P, 1], F32, name=f"sd{b}")
+            nc.vector.tensor_scalar_add(out=sd[:], in0=mv[:, 1:2], scalar1=1e-5)
+            sq = keep.tile([P, 1], F32, name=f"sq{b}")
+            nc.scalar.activation(out=sq[:], in_=sd[:], func=ACT.Sqrt)
+            stat[b] = (mv, sq)
+
+        def stats_spread(b):
+            mv, sq = stat[b]
+            rs = keep.tile([P, 1], F32, name=f"rs{b}")
+            nc.vector.reciprocal(out=rs[:], in_=sq[:])
+            bank = psum.tile([P, 2, P], F32, name="turned", bufs=3)
+            nc.tensor.matmul(bank[:, 0], lhsT=mv[:, 0:1].to_broadcast([P, P]), rhs=ident_f[:], start=True, stop=True)
+            nc.tensor.matmul(bank[:, 1], lhsT=rs[:].to_broadcast([P, P]), rhs=ident_f[:], start=True, stop=True)
+            mur[b] = keep.tile([P, 2, C], F32, name=f"mur{b}")
+            nc.scalar.copy(out=mur[b][:], in_=bank[:])
+
+        def normalise(c):
+            b, j = divmod(c, CPS)
+            d = pool.tile([P, CR, C], F32, name="d")
+            xn[c] = pool.tile([P, CR, C], F32, name="xn", bufs=3)
+            nc.gpsimd.tensor_tensor(
+                out=d[:], in0=x_sb[b][:, j * CR : (j + 1) * CR], in1=mur[b][:, 0:1].to_broadcast([P, CR, C]), op=ALU.subtract
+            )
+            nc.gpsimd.tensor_tensor(out=xn[c][:], in0=d[:], in1=mur[b][:, 1:2].to_broadcast([P, CR, C]), op=ALU.mult)
+
+        def modulate1(c):
+            t1 = pool.tile([P, CR, C], F32, name="t1")
+            nc.vector.scalar_tensor_tensor(
+                out=t1[:], in0=gb[c][0][:], scalar=1.0, in1=xn.pop(c)[:], op0=ALU.add, op1=ALU.mult
+            )
+            ep[("t1", c)] = t1
+
+        def modulate2(c):
+            y = pool.tile([P, CR, C], F32, name="y")
+            nc.vector.tensor_tensor(out=y[:], in0=gb.pop(c)[1][:], in1=ep.pop(("t1", c))[:], op=ALU.add)
+            ep[("y", c)] = y
+
+        def leaky(c):
+            b, j = divmod(c, CPS)
+            o = pool.tile([P, CR, C], F32, name="o", bufs=3)
+            y = ep.pop(("y", c))
+            nc.vector.scalar_tensor_tensor(out=o[:], in0=y[:], scalar=0.2, in1=y[:], op0=ALU.mult, op1=ALU.max)
+            nc.sync.dma_start(out=out_view[b][:, j * CR : (j + 1) * CR], in_=o[:])
+
+        def on(f, c, *rest):
+            if 0 <= c < NCH:
+                f(c, *rest)
+
+        for i in range(CR):
+            widen(0, i)
+        group_wm(0, "v")
+        group_wm(1, "g")
+        for s in range(NCH + 4):
+            if s % CPS == 1 and s < NCH:
+                stats_aggr(s // CPS)
+            on(interleave, s - 2)
+            on(normalise, s - 2)
+            on(turn, s, 0)
+            on(scale_up, s, 0)
+            on(widen, s + 1, 0)
+            on(turn, s, 1)
+            on(scale_up, s, 1)
+            on(maps, s - 3)
+            on(embed, s - 1, 0)
+            on(rectify, s - 1, 0)
+            on(widen, s + 1, 1)
+            on(embed, s - 1, 1)
+            on(rectify, s - 1, 1)
+            on(modulate1, s - 3)
+            on(turn, s, 2)
+            on(scale_up, s, 2)
+            if s == 0:
+                quantise_wm(0)
+                group_w2(0)
+            on(widen, s + 1, 2)
+            on(turn, s, 3)
+            on(scale_up, s, 3)
+            if s == 0:
+                quantise_wm(1)
+                group_w2(1)
+                quantise_w2()
+            on(embed, s - 1, 2)
+            on(rectify, s - 1, 2)
+            on(modulate2, s - 3)
+            on(quantise_m, s)
+            on(widen, s + 1, 3)
+            on(embed, s - 1, 3)
+            on(rectify, s - 1, 3)
+            on(leaky, s - 3)
+            on(quantise_a, s - 2)
+            if s % CPS == 0 and s < NCH:
+                stats_turn(s // CPS, 0)
+                stats_turn(s // CPS, 1)
+            if s % CPS == 1 and s < NCH:
+                stats_spread(s // CPS)

@@ -17,10 +17,8 @@ ACT = mybir.ActivationFunctionType
 
 P = 128
 ROWS = POS // P
-CR = 4
-NT = CR * P
-CPS = ROWS // CR
-NCH = B * CPS
+CHUNKS = [(b, r, 4) for b in range(B) for r in range(0, ROWS, 4)][:-1] + [(B - 1, 12, 2), (B - 1, 14, 2)]
+NCH = len(CHUNKS)
 G = S // 512
 
 
@@ -37,7 +35,7 @@ def tile_spademodulationpointwise_t_kernel(tc, x, m_bytes, m_scale, wm, bm, g, w
         out_view = out.rearrange("b (p i) c -> b p i c", i=ROWS)
         wm_view = wm.rearrange("(g p j) c -> g p (j c)", p=P, j=4)
 
-        codes_in = [keep.tile([P, CR * S], U8, name=f"codes_in{c}", align_bytes=64) for c in range(NCH)]
+        codes_in = [keep.tile([P, CHUNKS[c][2] * S], U8, name=f"codes_in{c}", align_bytes=64) for c in range(NCH)]
         x_sb = [keep.tile([P, ROWS, C], BF16, name=f"x_sb{b}", align_bytes=64) for b in range(B)]
         wm_raw = [keep.tile([P, 4 * K], BF16, name=f"wm_raw{i}", align_bytes=64) for i in range(G)]
         w2_raw = keep.tile([P, 2, 4, C], BF16, name="w2_raw", align_bytes=64)
@@ -46,11 +44,9 @@ def tile_spademodulationpointwise_t_kernel(tc, x, m_bytes, m_scale, wm, bm, g, w
         bias_raw = keep.tile([P, 4], BF16, name="bias_raw")
 
         def load_codes(c, i0, i1):
-            b, j = divmod(c, CPS)
-            nc.sync.dma_start(
-                out=codes_in[c][:, i0 * S : i1 * S],
-                in_=m_view[b][:, (j * CR + i0) * S : (j * CR + i1) * S],
-            )
+            b, r, n = CHUNKS[c]
+            i1 = min(i1, n)
+            nc.sync.dma_start(out=codes_in[c][:, i0 * S : i1 * S], in_=m_view[b][:, (r + i0) * S : (r + i1) * S])
 
         load_codes(0, 0, 1)
         load_codes(0, 1, 2)
@@ -66,8 +62,8 @@ def tile_spademodulationpointwise_t_kernel(tc, x, m_bytes, m_scale, wm, bm, g, w
         nc.sync.dma_start(out=x_sb[0][:], in_=x_view[0])
         for c in range(2, NCH):
             load_codes(c, 0, 4)
-            if c % CPS == 1 and c > 1:
-                nc.sync.dma_start(out=x_sb[c // CPS][:], in_=x_view[c // CPS])
+            if c % 4 == 1 and CHUNKS[c][2] == 4:
+                nc.sync.dma_start(out=x_sb[c // 4][:], in_=x_view[c // 4])
 
         warm = keep.tile([P, 1], F32, name="warm")
         nc.vector.memset(warm[:], 1.0)
@@ -119,7 +115,7 @@ def tile_spademodulationpointwise_t_kernel(tc, x, m_bytes, m_scale, wm, bm, g, w
 
         def widen(c, i):
             if i == 0:
-                wide[c] = pool.tile([P, CR * S], BF16, name="wide", align_bytes=64, bufs=2)
+                wide[c] = pool.tile([P, CHUNKS[c][2] * S], BF16, name="wide", align_bytes=64, bufs=2)
             cols = slice(i * S, (i + 1) * S)
             if c == 0 and i % 2 == 1:
                 nc.vector.tensor_copy(out=wide[c][:, cols], in_=codes_in[c][:, cols].bitcast(FP8))
@@ -127,7 +123,7 @@ def tile_spademodulationpointwise_t_kernel(tc, x, m_bytes, m_scale, wm, bm, g, w
                 nc.scalar.copy(out=wide[c][:, cols], in_=codes_in[c][:, cols].bitcast(FP8))
 
         def turn(c, k):
-            gg, h = divmod(k, 2)
+            gg, h = divmod(k, CHUNKS[c][2] // 2)
             words = wide[c][:].bitcast(F32)
             bank = psum.tile([P, 2, 256], F32, name="turned", bufs=3)
             for i2 in range(2):
@@ -138,9 +134,10 @@ def tile_spademodulationpointwise_t_kernel(tc, x, m_bytes, m_scale, wm, bm, g, w
             ep[("bank", c, k)] = bank
 
         def scale_up(c, k):
-            gg, h = divmod(k, 2)
+            n = CHUNKS[c][2]
+            gg, h = divmod(k, n // 2)
             if k == 0:
-                mgrp[c] = pool.tile([P, G, NT * 4], BF16, name="mgrp", align_bytes=64, bufs=2)
+                mgrp[c] = pool.tile([P, G, n * P * 4], BF16, name="mgrp", align_bytes=64, bufs=2)
             bank = ep.pop(("bank", c, k))
             src = bank[:].rearrange("p u r -> p (u r)").bitcast(BF16).rearrange("p (u r e) -> p r u e", u=2, e=2)
             dst = mgrp[c][:, gg, h * 1024 : (h + 1) * 1024].rearrange("p (r u e) -> p r u e", u=2, e=2)
@@ -148,18 +145,20 @@ def tile_spademodulationpointwise_t_kernel(tc, x, m_bytes, m_scale, wm, bm, g, w
             nc.vector.tensor_tensor(out=dst, in0=src, in1=sc, op=ALU.mult)
 
         def quantise_m(c):
-            codes = pool.tile([P, G * NT], U32, name="m_codes", align_bytes=64, bufs=2)
-            scales = pool.tile([P, G * NT], U8, name="m_scales", align_bytes=64, bufs=2)
+            n = CHUNKS[c][2] * P
+            codes = pool.tile([P, G * n], U32, name="m_codes", align_bytes=64, bufs=2)
+            scales = pool.tile([P, G * n], U8, name="m_scales", align_bytes=64, bufs=2)
             nc.vector.quantize_mx(
                 out=codes[:].bitcast(X4), scales=scales[:], in_=mgrp.pop(c)[:].rearrange("p g n -> p (g n)")
             )
             mq[c] = (codes, scales)
 
         def embed(c, t):
-            h = psum.tile([P, NT], F32, name="embed", bufs=3)
+            n = CHUNKS[c][2] * P
+            h = psum.tile([P, n], F32, name="embed", bufs=3)
             for gg in range(G):
                 codes, scales = mq[c]
-                tok = slice(gg * NT, (gg + 1) * NT)
+                tok = slice(gg * n, (gg + 1) * n)
                 cols = slice(t * P, (t + 1) * P)
                 nc.tensor.matmul_mx(
                     out=h[:],
@@ -174,22 +173,28 @@ def tile_spademodulationpointwise_t_kernel(tc, x, m_bytes, m_scale, wm, bm, g, w
 
         def rectify(c, t):
             if t == 0:
-                apl[c] = pool.tile([P, 4, NT], BF16, name="apl", align_bytes=64, bufs=2)
+                apl[c] = pool.tile([P, 4, CHUNKS[c][2] * P], BF16, name="apl", align_bytes=64, bufs=2)
             nc.scalar.activation(
                 out=apl[c][:, t], in_=hp.pop((c, t))[:], func=ACT.Relu, bias=bias4[:, t : t + 1], scale=gain4[:, t : t + 1]
             )
 
         def interleave(c):
-            agrp[c] = pool.tile([P, NT, 4], BF16, name="agrp", align_bytes=64, bufs=2)
+            n = CHUNKS[c][2]
+            agrp[c] = pool.tile([P, n * P, 4], BF16, name="agrp", align_bytes=64, bufs=2)
             src = apl.pop(c)[:].rearrange("p t n -> p n t")
-            if c == NCH - 1:
+            if c >= NCH - 2:
                 nc.vector.tensor_copy(out=agrp[c][:], in_=src)
             else:
-                nc.gpsimd.tensor_scalar(out=agrp[c][:], in0=src, scalar1=1.0, scalar2=0.0, op0=ALU.mult, op1=ALU.add)
+                for i in range(n):
+                    tok = slice(i * P, (i + 1) * P)
+                    nc.gpsimd.tensor_scalar(
+                        out=agrp[c][:, tok], in0=src[:, tok], scalar1=1.0, scalar2=0.0, op0=ALU.mult, op1=ALU.add
+                    )
 
         def quantise_a(c):
-            codes = pool.tile([P, NT], U32, name="a_codes", align_bytes=64, bufs=2)
-            scales = pool.tile([P, NT], U8, name="a_scales", align_bytes=64, bufs=2)
+            n = CHUNKS[c][2] * P
+            codes = pool.tile([P, n], U32, name="a_codes", align_bytes=64, bufs=2)
+            scales = pool.tile([P, n], U8, name="a_scales", align_bytes=64, bufs=2)
             nc.vector.quantize_mx(
                 out=codes[:].bitcast(X4), scales=scales[:], in_=agrp.pop(c)[:].rearrange("p n t -> p (n t)")
             )
@@ -197,9 +202,10 @@ def tile_spademodulationpointwise_t_kernel(tc, x, m_bytes, m_scale, wm, bm, g, w
 
         def maps(c):
             codes, scales = aq.pop(c)
-            gam = psum.tile([P, CR, C], F32, name="gam", bufs=1)
-            bet = psum.tile([P, CR, C], F32, name="bet", bufs=1)
-            for i in range(CR):
+            n = CHUNKS[c][2]
+            gam = psum.tile([P, n, C], F32, name="gam", bufs=1)
+            bet = psum.tile([P, n, C], F32, name="bet", bufs=1)
+            for i in range(n):
                 cols = slice(i * P, (i + 1) * P)
                 for w, dst in ((0, gam), (1, bet)):
                     wc = slice(w * C, (w + 1) * C)
@@ -243,44 +249,51 @@ def tile_spademodulationpointwise_t_kernel(tc, x, m_bytes, m_scale, wm, bm, g, w
             nc.scalar.copy(out=mur[b][:], in_=bank[:])
 
         def normalise(c):
-            b, j = divmod(c, CPS)
-            d = pool.tile([P, CR, C], F32, name="d")
-            xn[c] = pool.tile([P, CR, C], F32, name="xn", bufs=3)
-            nc.gpsimd.tensor_tensor(
-                out=d[:], in0=x_sb[b][:, j * CR : (j + 1) * CR], in1=mur[b][:, 0:1].to_broadcast([P, CR, C]), op=ALU.subtract
-            )
-            nc.gpsimd.tensor_tensor(out=xn[c][:], in0=d[:], in1=mur[b][:, 1:2].to_broadcast([P, CR, C]), op=ALU.mult)
+            b, r, n = CHUNKS[c]
+            d = pool.tile([P, n, C], F32, name="d")
+            xn[c] = pool.tile([P, n, C], F32, name="xn", bufs=3)
+            mu, rs = (mur[b][:, q : q + 1].to_broadcast([P, 2, C]) for q in range(2))
+            for i in range(0, n, 2):
+                two = slice(i, i + 2)
+                nc.gpsimd.tensor_tensor(out=d[:, two], in0=x_sb[b][:, r + i : r + i + 2], in1=mu, op=ALU.subtract)
+            for i in range(0, n, 2):
+                two = slice(i, i + 2)
+                nc.gpsimd.tensor_tensor(out=xn[c][:, two], in0=d[:, two], in1=rs, op=ALU.mult)
 
         def modulate1(c):
-            t1 = pool.tile([P, CR, C], F32, name="t1")
+            t1 = pool.tile([P, CHUNKS[c][2], C], F32, name="t1")
             nc.vector.scalar_tensor_tensor(
                 out=t1[:], in0=gb[c][0][:], scalar=1.0, in1=xn.pop(c)[:], op0=ALU.add, op1=ALU.mult
             )
             ep[("t1", c)] = t1
 
         def modulate2(c):
-            y = pool.tile([P, CR, C], F32, name="y")
+            y = pool.tile([P, CHUNKS[c][2], C], F32, name="y")
             nc.vector.tensor_tensor(out=y[:], in0=gb.pop(c)[1][:], in1=ep.pop(("t1", c))[:], op=ALU.add)
             ep[("y", c)] = y
 
         def leaky(c):
-            b, j = divmod(c, CPS)
-            o = pool.tile([P, CR, C], F32, name="o", bufs=3)
+            b, r, n = CHUNKS[c]
+            o = pool.tile([P, n, C], F32, name="o", bufs=3)
             y = ep.pop(("y", c))
             nc.vector.scalar_tensor_tensor(out=o[:], in0=y[:], scalar=0.2, in1=y[:], op0=ALU.mult, op1=ALU.max)
-            nc.sync.dma_start(out=out_view[b][:, j * CR : (j + 1) * CR], in_=o[:])
+            nc.sync.dma_start(out=out_view[b][:, r : r + n], in_=o[:])
 
         def on(f, c, *rest):
             if 0 <= c < NCH:
+                if f in (widen, turn, scale_up) and rest[0] >= CHUNKS[c][2]:
+                    return
                 f(c, *rest)
 
-        for i in range(CR):
+        for i in range(4):
             widen(0, i)
         group_wm(0, "v")
         group_wm(1, "g")
-        for s in range(NCH + 4):
-            if s % CPS == 1 and s < NCH:
-                stats_aggr(s // CPS)
+        for s in range(NCH + 3):
+            first = s % 4 == 0 and s < 4 * B
+            second = s % 4 == 1 and s < 4 * B
+            if second:
+                stats_aggr(s // 4)
             on(interleave, s - 2)
             on(normalise, s - 2)
             on(turn, s, 0)
@@ -288,36 +301,35 @@ def tile_spademodulationpointwise_t_kernel(tc, x, m_bytes, m_scale, wm, bm, g, w
             on(widen, s + 1, 0)
             on(turn, s, 1)
             on(scale_up, s, 1)
-            on(maps, s - 3)
             on(embed, s - 1, 0)
             on(rectify, s - 1, 0)
+            on(maps, s - 3)
             on(widen, s + 1, 1)
+            on(turn, s, 2)
+            on(modulate1, s - 3)
+            on(scale_up, s, 2)
             on(embed, s - 1, 1)
             on(rectify, s - 1, 1)
-            on(modulate1, s - 3)
-            on(turn, s, 2)
-            on(scale_up, s, 2)
-            if s == 0:
-                quantise_wm(0)
-                group_w2(0)
             on(widen, s + 1, 2)
             on(turn, s, 3)
             on(scale_up, s, 3)
+            on(embed, s - 1, 2)
+            on(rectify, s - 1, 2)
+            on(widen, s + 1, 3)
+            on(modulate2, s - 3)
             if s == 0:
+                quantise_wm(0)
+                group_w2(0)
                 quantise_wm(1)
                 group_w2(1)
                 quantise_w2()
-            on(embed, s - 1, 2)
-            on(rectify, s - 1, 2)
-            on(modulate2, s - 3)
+            on(quantise_a, s - 2)
             on(quantise_m, s)
-            on(widen, s + 1, 3)
             on(embed, s - 1, 3)
             on(rectify, s - 1, 3)
             on(leaky, s - 3)
-            on(quantise_a, s - 2)
-            if s % CPS == 0 and s < NCH:
-                stats_turn(s // CPS, 0)
-                stats_turn(s // CPS, 1)
-            if s % CPS == 1 and s < NCH:
-                stats_spread(s // CPS)
+            if first:
+                stats_turn(s // 4, 0)
+                stats_turn(s // 4, 1)
+            if second:
+                stats_spread(s // 4)

@@ -55,15 +55,17 @@ def tile_spademodulationpointwise_t_kernel(tc, x, m_bytes, m_scale, wm, bm, g, w
         nc.scalar.dma_start(out=bias_raw[:], in_=bm.rearrange("(p t) -> p t", t=4))
         nc.sync.dma_start(out=wm_raw[0][:], in_=wm_view[0])
         load_codes(0, 2, 4)
+        load_codes(1, 0, 2)
         nc.sync.dma_start(out=wm_raw[1][:], in_=wm_view[1])
-        load_codes(1, 0, 4)
+        nc.sync.dma_start(out=x_sb[0][:], in_=x_view[0])
+        load_codes(1, 2, 4)
         nc.sync.dma_start(out=w2_raw[:, 0], in_=wg.rearrange("(p j) c -> p j c", j=4))
         nc.sync.dma_start(out=w2_raw[:, 1], in_=wb.rearrange("(p j) c -> p j c", j=4))
-        nc.sync.dma_start(out=x_sb[0][:], in_=x_view[0])
         for c in range(2, NCH):
             load_codes(c, 0, 4)
-            if c % 4 == 1 and CHUNKS[c][2] == 4:
-                nc.sync.dma_start(out=x_sb[c // 4][:], in_=x_view[c // 4])
+            if c in (2, 4, 8):
+                b = {2: 1, 4: 2, 8: 3}[c]
+                nc.sync.dma_start(out=x_sb[b][:], in_=x_view[b])
 
         warm = keep.tile([P, 1], F32, name="warm")
         nc.vector.memset(warm[:], 1.0)
@@ -72,6 +74,8 @@ def tile_spademodulationpointwise_t_kernel(tc, x, m_bytes, m_scale, wm, bm, g, w
         make_identity(nc, ident_f[:])
         ident_b = keep.tile([P, P], BF16, name="ident_b")
         nc.vector.tensor_copy(out=ident_b[:], in_=ident_f[:])
+        ones = keep.tile([P, 64], BF16, name="ones")
+        nc.vector.memset(ones[:], 1.0)
         sign4 = keep.tile([P, 4], F32, name="sign4")
         gain4 = keep.tile([P, 4], F32, name="gain4")
         bias4 = keep.tile([P, 4], F32, name="bias4")
@@ -99,7 +103,7 @@ def tile_spademodulationpointwise_t_kernel(tc, x, m_bytes, m_scale, wm, bm, g, w
             nc.vector.quantize_mx(out=wm_codes[i][:].bitcast(X4), scales=wm_scales[i][:], in_=wm_grp[i][:])
 
         def group_w2(w):
-            nc.vector.tensor_tensor(
+            nc.gpsimd.tensor_tensor(
                 out=w2_grp[:, w],
                 in0=w2_raw[:, w].rearrange("p j c -> p c j"),
                 in1=sign4[:].unsqueeze(1).to_broadcast([P, C, 4]),
@@ -115,15 +119,15 @@ def tile_spademodulationpointwise_t_kernel(tc, x, m_bytes, m_scale, wm, bm, g, w
 
         def widen(c, i):
             if i == 0:
-                wide[c] = pool.tile([P, CHUNKS[c][2] * S], BF16, name="wide", align_bytes=64, bufs=2)
+                wide[c] = pool.tile([P, CHUNKS[c][2] * S], BF16, name="wide", align_bytes=64, bufs=3)
             cols = slice(i * S, (i + 1) * S)
-            if c == 0 and i % 2 == 1:
+            if c in (0, 3) and i % 2 == 1:
                 nc.vector.tensor_copy(out=wide[c][:, cols], in_=codes_in[c][:, cols].bitcast(FP8))
             else:
                 nc.scalar.copy(out=wide[c][:, cols], in_=codes_in[c][:, cols].bitcast(FP8))
 
         def turn(c, k):
-            gg, h = divmod(k, CHUNKS[c][2] // 2)
+            h, gg = divmod(k, G)
             words = wide[c][:].bitcast(F32)
             bank = psum.tile([P, 2, 256], F32, name="turned", bufs=3)
             for i2 in range(2):
@@ -135,7 +139,7 @@ def tile_spademodulationpointwise_t_kernel(tc, x, m_bytes, m_scale, wm, bm, g, w
 
         def scale_up(c, k):
             n = CHUNKS[c][2]
-            gg, h = divmod(k, n // 2)
+            h, gg = divmod(k, G)
             if k == 0:
                 mgrp[c] = pool.tile([P, G, n * P * 4], BF16, name="mgrp", align_bytes=64, bufs=2)
             bank = ep.pop(("bank", c, k))
@@ -155,7 +159,7 @@ def tile_spademodulationpointwise_t_kernel(tc, x, m_bytes, m_scale, wm, bm, g, w
 
         def embed(c, t):
             n = CHUNKS[c][2] * P
-            h = psum.tile([P, n], F32, name="embed", bufs=3)
+            h = psum.tile([P, n], F32, name="embed", bufs=2)
             for gg in range(G):
                 codes, scales = mq[c]
                 tok = slice(gg * n, (gg + 1) * n)
@@ -180,16 +184,12 @@ def tile_spademodulationpointwise_t_kernel(tc, x, m_bytes, m_scale, wm, bm, g, w
 
         def interleave(c):
             n = CHUNKS[c][2]
-            agrp[c] = pool.tile([P, n * P, 4], BF16, name="agrp", align_bytes=64, bufs=2)
+            agrp[c] = pool.tile([P, n * P, 4], BF16, name="agrp", align_bytes=64, bufs=1)
             src = apl.pop(c)[:].rearrange("p t n -> p n t")
-            if c >= NCH - 2:
+            if c >= NCH - 3:
                 nc.vector.tensor_copy(out=agrp[c][:], in_=src)
             else:
-                for i in range(n):
-                    tok = slice(i * P, (i + 1) * P)
-                    nc.gpsimd.tensor_scalar(
-                        out=agrp[c][:, tok], in0=src[:, tok], scalar1=1.0, scalar2=0.0, op0=ALU.mult, op1=ALU.add
-                    )
+                nc.gpsimd.tensor_scalar(out=agrp[c][:], in0=src, scalar1=1.0, scalar2=0.0, op0=ALU.mult, op1=ALU.add)
 
         def quantise_a(c):
             n = CHUNKS[c][2] * P
@@ -220,45 +220,55 @@ def tile_spademodulationpointwise_t_kernel(tc, x, m_bytes, m_scale, wm, bm, g, w
                     )
             gb[c] = (gam, bet)
 
-        def stats_turn(b, h):
-            if h == 0:
-                stat[b] = keep.tile([P, 4, 6], F32, name=f"bnst{b}")
-            bank = psum.tile([P, 8, P], BF16, name="turned", bufs=3)
-            for i in range(8):
-                nc.tensor.transpose(bank[:, i], x_sb[b][:, h * 8 + i], ident_b[:])
-            for q in range(2):
-                nc.vector.bn_stats(out=stat[b][:, 2 * h + q], in_=bank[:, 4 * q : 4 * q + 4].rearrange("p i c -> p (i c)"))
+        def stats_mean(b):
+            bank = psum.tile([P, 64], F32, name="spare", bufs=1)
+            for i in range(ROWS):
+                nc.tensor.matmul(bank[:], lhsT=x_sb[b][:, i], rhs=ones[:], start=(i == 0), stop=(i == ROWS - 1))
+            neg_mean = keep.tile([P, 1], F32, name=f"neg_mean{b}")
+            nc.vector.tensor_scalar(out=neg_mean[:], in0=bank[:, 0:1], scalar1=-1.0 / POS, scalar2=None, op0=ALU.mult)
+            stat[b] = [neg_mean, keep.tile([P, 4], F32, name=f"squares{b}")]
 
-        def stats_aggr(b):
-            mv = keep.tile([P, 2], F32, name=f"mv{b}")
-            nc.vector.bn_aggr(out=mv[:], in_=stat[b][:].rearrange("p a s -> p (a s)"))
-            sd = keep.tile([P, 1], F32, name=f"sd{b}")
-            nc.vector.tensor_scalar_add(out=sd[:], in0=mv[:, 1:2], scalar1=1e-5)
-            sq = keep.tile([P, 1], F32, name=f"sq{b}")
-            nc.scalar.activation(out=sq[:], in_=sd[:], func=ACT.Sqrt)
-            stat[b] = (mv, sq)
+        def stats_squares(b, h):
+            bank = psum.tile([P, 4, P], BF16, name="spare", bufs=1)
+            for i in range(4):
+                nc.tensor.transpose(bank[:, i], x_sb[b][:, h * 4 + i], ident_b[:])
+            junk = pool.tile([P, 4, P], BF16, name="junk")
+            neg_mean, squares = stat[b]
+            nc.scalar.activation(
+                out=junk[:], in_=bank[:], func=ACT.Square, bias=neg_mean[:], accum_out=squares[:, h : h + 1]
+            )
+
+        def stats_sqrt(b):
+            neg_mean, squares = stat[b]
+            total = keep.tile([P, 1], F32, name=f"total{b}")
+            nc.vector.tensor_reduce(out=total[:], in_=squares[:], axis=mybir.AxisListType.X, op=ALU.add)
+            var = keep.tile([P, 1], F32, name=f"var{b}")
+            nc.vector.tensor_scalar(out=var[:], in0=total[:], scalar1=1.0 / POS, scalar2=1e-5, op0=ALU.mult, op1=ALU.add)
+            std = keep.tile([P, 1], F32, name=f"std{b}")
+            nc.scalar.activation(out=std[:], in_=var[:], func=ACT.Sqrt)
+            stat[b] = (neg_mean, std)
+
+        def stats_rstd(b):
+            neg_mean, std = stat[b]
+            rstd = keep.tile([P, 1], F32, name=f"rstd{b}")
+            nc.vector.reciprocal(out=rstd[:], in_=std[:])
+            stat[b] = (neg_mean, rstd)
 
         def stats_spread(b):
-            mv, sq = stat[b]
-            rs = keep.tile([P, 1], F32, name=f"rs{b}")
-            nc.vector.reciprocal(out=rs[:], in_=sq[:])
-            bank = psum.tile([P, 2, P], F32, name="turned", bufs=3)
-            nc.tensor.matmul(bank[:, 0], lhsT=mv[:, 0:1].to_broadcast([P, P]), rhs=ident_f[:], start=True, stop=True)
-            nc.tensor.matmul(bank[:, 1], lhsT=rs[:].to_broadcast([P, P]), rhs=ident_f[:], start=True, stop=True)
+            neg_mean, rstd = stat[b]
+            bank = psum.tile([P, 2, P], F32, name="spare", bufs=1)
+            nc.tensor.matmul(bank[:, 0], lhsT=neg_mean[:].to_broadcast([P, P]), rhs=ident_f[:], start=True, stop=True)
+            nc.tensor.matmul(bank[:, 1], lhsT=rstd[:].to_broadcast([P, P]), rhs=ident_f[:], start=True, stop=True)
             mur[b] = keep.tile([P, 2, C], F32, name=f"mur{b}")
             nc.scalar.copy(out=mur[b][:], in_=bank[:])
 
         def normalise(c):
             b, r, n = CHUNKS[c]
             d = pool.tile([P, n, C], F32, name="d")
-            xn[c] = pool.tile([P, n, C], F32, name="xn", bufs=3)
-            mu, rs = (mur[b][:, q : q + 1].to_broadcast([P, 2, C]) for q in range(2))
-            for i in range(0, n, 2):
-                two = slice(i, i + 2)
-                nc.gpsimd.tensor_tensor(out=d[:, two], in0=x_sb[b][:, r + i : r + i + 2], in1=mu, op=ALU.subtract)
-            for i in range(0, n, 2):
-                two = slice(i, i + 2)
-                nc.gpsimd.tensor_tensor(out=xn[c][:, two], in0=d[:, two], in1=rs, op=ALU.mult)
+            xn[c] = pool.tile([P, n, C], F32, name="xn", bufs=5)
+            mu, rs = (mur[b][:, q : q + 1].to_broadcast([P, n, C]) for q in range(2))
+            nc.gpsimd.tensor_tensor(out=d[:], in0=x_sb[b][:, r : r + n], in1=mu, op=ALU.add)
+            nc.gpsimd.tensor_tensor(out=xn[c][:], in0=d[:], in1=rs, op=ALU.mult)
 
         def modulate1(c):
             t1 = pool.tile([P, CHUNKS[c][2], C], F32, name="t1")
@@ -290,46 +300,66 @@ def tile_spademodulationpointwise_t_kernel(tc, x, m_bytes, m_scale, wm, bm, g, w
         group_wm(0, "v")
         group_wm(1, "g")
         for s in range(NCH + 3):
-            first = s % 4 == 0 and s < 4 * B
-            second = s % 4 == 1 and s < 4 * B
-            if second:
-                stats_aggr(s // 4)
-            on(interleave, s - 2)
-            on(normalise, s - 2)
+            nxt, q = divmod(s + 4, 4)
+            if q == 0 and 4 <= s < 4 * B:
+                stats_rstd(s // 4)
             on(turn, s, 0)
+            on(interleave, s - 2)
             on(scale_up, s, 0)
-            on(widen, s + 1, 0)
+            on(widen, s + 2, 0)
             on(turn, s, 1)
             on(scale_up, s, 1)
             on(embed, s - 1, 0)
             on(rectify, s - 1, 0)
+            on(widen, s + 2, 1)
             on(maps, s - 3)
-            on(widen, s + 1, 1)
-            on(turn, s, 2)
             on(modulate1, s - 3)
+            if q == 0 and 4 <= s < 4 * B:
+                stats_spread(s // 4)
+            on(turn, s, 2)
             on(scale_up, s, 2)
+            if nxt < B and q == 0 and s > 0 or s == 1:
+                stats_mean(nxt)
             on(embed, s - 1, 1)
             on(rectify, s - 1, 1)
-            on(widen, s + 1, 2)
+            on(widen, s + 2, 2)
+            on(modulate2, s - 3)
+            if s == 1:
+                stats_sqrt(0)
+            if s == 1:
+                stats_squares(1, 0)
+            if nxt < B and s > 0:
+                stats_squares(nxt, q)
             on(turn, s, 3)
             on(scale_up, s, 3)
+            if s == 0:
+                stats_mean(0)
+                for i in range(4):
+                    stats_squares(0, i)
+                    widen(1, i)
             on(embed, s - 1, 2)
             on(rectify, s - 1, 2)
-            on(widen, s + 1, 3)
-            on(modulate2, s - 3)
+            on(widen, s + 2, 3)
             if s == 0:
                 quantise_wm(0)
-                group_w2(0)
                 quantise_wm(1)
+            if s == 1:
+                stats_rstd(0)
+                group_w2(0)
                 group_w2(1)
+            if s == 2:
                 quantise_w2()
-            on(quantise_a, s - 2)
-            on(quantise_m, s)
             on(embed, s - 1, 3)
             on(rectify, s - 1, 3)
+            if nxt < B and q == 3:
+                stats_sqrt(nxt)
+            if s == 1:
+                stats_spread(0)
             on(leaky, s - 3)
-            if first:
-                stats_turn(s // 4, 0)
-                stats_turn(s // 4, 1)
-            if second:
-                stats_spread(s // 4)
+            on(quantise_m, s)
+            on(quantise_a, s - 2)
+            if s < NCH:
+                on(normalise, s - 2)
+            if s == NCH - 1:
+                normalise(NCH - 2)
+                normalise(NCH - 1)

@@ -121,7 +121,7 @@ def tile_spademodulationpointwise_t_kernel(tc, x, m_bytes, m_scale, wm, bm, g, w
             if i == 0:
                 wide[c] = pool.tile([P, CHUNKS[c][2] * S], BF16, name="wide", align_bytes=64, bufs=3)
             cols = slice(i * S, (i + 1) * S)
-            if c in (0, 3) and i % 2 == 1:
+            if c == 0 and i % 2 == 1:
                 nc.vector.tensor_copy(out=wide[c][:, cols], in_=codes_in[c][:, cols].bitcast(FP8))
             else:
                 nc.scalar.copy(out=wide[c][:, cols], in_=codes_in[c][:, cols].bitcast(FP8))
@@ -159,7 +159,7 @@ def tile_spademodulationpointwise_t_kernel(tc, x, m_bytes, m_scale, wm, bm, g, w
 
         def embed(c, t):
             n = CHUNKS[c][2] * P
-            h = psum.tile([P, n], F32, name="embed", bufs=2)
+            h = psum.tile([P, n], F32, name="embed", bufs=3)
             for gg in range(G):
                 codes, scales = mq[c]
                 tok = slice(gg * n, (gg + 1) * n)
@@ -187,7 +187,7 @@ def tile_spademodulationpointwise_t_kernel(tc, x, m_bytes, m_scale, wm, bm, g, w
             agrp[c] = pool.tile([P, n * P, 4], BF16, name="agrp", align_bytes=64, bufs=1)
             src = apl.pop(c)[:].rearrange("p t n -> p n t")
             if c >= NCH - 3:
-                nc.vector.tensor_copy(out=agrp[c][:], in_=src)
+                nc.scalar.copy(out=agrp[c][:], in_=src)
             else:
                 nc.gpsimd.tensor_scalar(out=agrp[c][:], in0=src, scalar1=1.0, scalar2=0.0, op0=ALU.mult, op1=ALU.add)
 
@@ -221,15 +221,15 @@ def tile_spademodulationpointwise_t_kernel(tc, x, m_bytes, m_scale, wm, bm, g, w
             gb[c] = (gam, bet)
 
         def stats_mean(b):
-            bank = psum.tile([P, 64], F32, name="spare", bufs=1)
+            bank = psum.tile([P, 64], F32, name="turned", bufs=3)
             for i in range(ROWS):
                 nc.tensor.matmul(bank[:], lhsT=x_sb[b][:, i], rhs=ones[:], start=(i == 0), stop=(i == ROWS - 1))
             neg_mean = keep.tile([P, 1], F32, name=f"neg_mean{b}")
-            nc.vector.tensor_scalar(out=neg_mean[:], in0=bank[:, 0:1], scalar1=-1.0 / POS, scalar2=None, op0=ALU.mult)
+            nc.scalar.mul(neg_mean[:], bank[:, 0:1], -1.0 / POS)
             stat[b] = [neg_mean, keep.tile([P, 4], F32, name=f"squares{b}")]
 
         def stats_squares(b, h):
-            bank = psum.tile([P, 4, P], BF16, name="spare", bufs=1)
+            bank = psum.tile([P, 4, P], BF16, name="turned", bufs=3)
             for i in range(4):
                 nc.tensor.transpose(bank[:, i], x_sb[b][:, h * 4 + i], ident_b[:])
             junk = pool.tile([P, 4, P], BF16, name="junk")
@@ -256,25 +256,28 @@ def tile_spademodulationpointwise_t_kernel(tc, x, m_bytes, m_scale, wm, bm, g, w
 
         def stats_spread(b):
             neg_mean, rstd = stat[b]
-            bank = psum.tile([P, 2, P], F32, name="spare", bufs=1)
+            bank = psum.tile([P, 2, P], F32, name="turned", bufs=3)
             nc.tensor.matmul(bank[:, 0], lhsT=neg_mean[:].to_broadcast([P, P]), rhs=ident_f[:], start=True, stop=True)
             nc.tensor.matmul(bank[:, 1], lhsT=rstd[:].to_broadcast([P, P]), rhs=ident_f[:], start=True, stop=True)
             mur[b] = keep.tile([P, 2, C], F32, name=f"mur{b}")
             nc.scalar.copy(out=mur[b][:], in_=bank[:])
 
-        def normalise(c):
-            b, r, n = CHUNKS[c]
-            d = pool.tile([P, n, C], F32, name="d")
-            xn[c] = pool.tile([P, n, C], F32, name="xn", bufs=5)
-            mu, rs = (mur[b][:, q : q + 1].to_broadcast([P, n, C]) for q in range(2))
-            nc.gpsimd.tensor_tensor(out=d[:], in0=x_sb[b][:, r : r + n], in1=mu, op=ALU.add)
-            nc.gpsimd.tensor_tensor(out=xn[c][:], in0=d[:], in1=rs, op=ALU.mult)
+        def centre(h):
+            b, r = h // 2, h % 2 * 8
+            xn[h] = pool.tile([P, 8, C], F32, name="xn", bufs=3)
+            nc.gpsimd.tensor_tensor(
+                out=xn[h][:], in0=x_sb[b][:, r : r + 8], in1=mur[b][:, 0:1].to_broadcast([P, 8, C]), op=ALU.add
+            )
+
+        def normalise(h):
+            rstd = mur[h // 2][:, 1:2].to_broadcast([P, 8, C])
+            nc.gpsimd.tensor_tensor(out=xn[h][:], in0=xn[h][:], in1=rstd, op=ALU.mult)
 
         def modulate1(c):
-            t1 = pool.tile([P, CHUNKS[c][2], C], F32, name="t1")
-            nc.vector.scalar_tensor_tensor(
-                out=t1[:], in0=gb[c][0][:], scalar=1.0, in1=xn.pop(c)[:], op0=ALU.add, op1=ALU.mult
-            )
+            b, r, n = CHUNKS[c]
+            t1 = pool.tile([P, n, C], F32, name="t1")
+            rows = xn[2 * b + r // 8][:, r % 8 : r % 8 + n]
+            nc.vector.scalar_tensor_tensor(out=t1[:], in0=gb[c][0][:], scalar=1.0, in1=rows, op0=ALU.add, op1=ALU.mult)
             ep[("t1", c)] = t1
 
         def modulate2(c):
@@ -295,71 +298,67 @@ def tile_spademodulationpointwise_t_kernel(tc, x, m_bytes, m_scale, wm, bm, g, w
                     return
                 f(c, *rest)
 
-        for i in range(4):
-            widen(0, i)
+        for c in range(2):
+            for i in range(4):
+                widen(c, i)
         group_wm(0, "v")
         group_wm(1, "g")
+        group_w2(0)
+        group_w2(1)
         for s in range(NCH + 3):
-            nxt, q = divmod(s + 4, 4)
-            if q == 0 and 4 <= s < 4 * B:
-                stats_rstd(s // 4)
+            b, q = divmod(s + 3, 4)
+            done = (s - 1) // 4
             on(turn, s, 0)
             on(interleave, s - 2)
             on(scale_up, s, 0)
-            on(widen, s + 2, 0)
+            if s:
+                on(widen, s + 1, 0)
             on(turn, s, 1)
             on(scale_up, s, 1)
+            if q == 0 and done < B:
+                stats_rstd(done)
             on(embed, s - 1, 0)
             on(rectify, s - 1, 0)
-            on(widen, s + 2, 1)
+            if s:
+                on(widen, s + 1, 1)
             on(maps, s - 3)
             on(modulate1, s - 3)
-            if q == 0 and 4 <= s < 4 * B:
-                stats_spread(s // 4)
             on(turn, s, 2)
+            if q == 0 and done < B:
+                stats_spread(done)
             on(scale_up, s, 2)
-            if nxt < B and q == 0 and s > 0 or s == 1:
-                stats_mean(nxt)
+            if 1 <= b < B and q == 0:
+                stats_mean(b)
             on(embed, s - 1, 1)
             on(rectify, s - 1, 1)
-            on(widen, s + 2, 2)
+            if s:
+                on(widen, s + 1, 2)
             on(modulate2, s - 3)
-            if s == 1:
-                stats_sqrt(0)
-            if s == 1:
-                stats_squares(1, 0)
-            if nxt < B and s > 0:
-                stats_squares(nxt, q)
+            if 1 <= b < B:
+                stats_squares(b, q)
             on(turn, s, 3)
             on(scale_up, s, 3)
             if s == 0:
                 stats_mean(0)
                 for i in range(4):
                     stats_squares(0, i)
-                    widen(1, i)
             on(embed, s - 1, 2)
             on(rectify, s - 1, 2)
-            on(widen, s + 2, 3)
+            if s:
+                on(widen, s + 1, 3)
             if s == 0:
                 quantise_wm(0)
                 quantise_wm(1)
-            if s == 1:
-                stats_rstd(0)
-                group_w2(0)
-                group_w2(1)
             if s == 2:
                 quantise_w2()
             on(embed, s - 1, 3)
             on(rectify, s - 1, 3)
-            if nxt < B and q == 3:
-                stats_sqrt(nxt)
-            if s == 1:
-                stats_spread(0)
             on(leaky, s - 3)
             on(quantise_m, s)
             on(quantise_a, s - 2)
-            if s < NCH:
-                on(normalise, s - 2)
-            if s == NCH - 1:
-                normalise(NCH - 2)
-                normalise(NCH - 1)
+            if s == 0:
+                stats_sqrt(0)
+            if 1 <= b < B and q == 3:
+                stats_sqrt(b)
+            if 0 < s < 17:
+                (centre if s % 2 else normalise)((s - 1) // 2)

@@ -16,10 +16,15 @@ ALU = mybir.AluOpType
 ACT = mybir.ActivationFunctionType
 
 P = 128
+PACK = 4
+PASSES = S // (P * PACK)
 ROWS = POS // P
+HALF = ROWS // 2
+
 CHUNKS = [(b, r, 4) for b in range(B) for r in range(0, ROWS, 4)][:-1] + [(B - 1, 12, 2), (B - 1, 14, 2)]
 NCH = len(CHUNKS)
-G = S // 512
+SCALAR_INTERLEAVES_FROM = NCH - 3
+X_BEHIND = {1: 2, 2: 4, 3: 8}
 
 
 def tile_spademodulationpointwise_t_kernel(tc, x, m_bytes, m_scale, wm, bm, g, wg, wb, out):
@@ -33,15 +38,15 @@ def tile_spademodulationpointwise_t_kernel(tc, x, m_bytes, m_scale, wm, bm, g, w
         m_view = m_bytes.rearrange("b (p i) k -> b p (i k)", i=ROWS)
         x_view = x.rearrange("b (p i) c -> b p i c", i=ROWS)
         out_view = out.rearrange("b (p i) c -> b p i c", i=ROWS)
-        wm_view = wm.rearrange("(g p j) c -> g p (j c)", p=P, j=4)
+        wm_view = wm.rearrange("(g p j) c -> g p (j c)", p=P, j=PACK)
 
         codes_in = [keep.tile([P, CHUNKS[c][2] * S], U8, name=f"codes_in{c}", align_bytes=64) for c in range(NCH)]
         x_sb = [keep.tile([P, ROWS, C], BF16, name=f"x_sb{b}", align_bytes=64) for b in range(B)]
-        wm_raw = [keep.tile([P, 4 * K], BF16, name=f"wm_raw{i}", align_bytes=64) for i in range(G)]
-        w2_raw = keep.tile([P, 2, 4, C], BF16, name="w2_raw", align_bytes=64)
-        scale4 = keep.tile([P, G, 4], F32, name="scale4")
-        gain_raw = keep.tile([P, 4], BF16, name="gain_raw")
-        bias_raw = keep.tile([P, 4], BF16, name="bias_raw")
+        wm_raw = [keep.tile([P, PACK * K], BF16, name=f"wm_raw{i}", align_bytes=64) for i in range(PASSES)]
+        w2_raw = keep.tile([P, 2, PACK, C], BF16, name="w2_raw", align_bytes=64)
+        scale4 = keep.tile([P, PASSES, PACK], F32, name="scale4")
+        gain_raw = keep.tile([P, PACK], BF16, name="gain_raw")
+        bias_raw = keep.tile([P, PACK], BF16, name="bias_raw")
 
         def load_codes(c, i0, i1):
             b, r, n = CHUNKS[c]
@@ -50,22 +55,22 @@ def tile_spademodulationpointwise_t_kernel(tc, x, m_bytes, m_scale, wm, bm, g, w
 
         load_codes(0, 0, 1)
         load_codes(0, 1, 2)
-        nc.scalar.dma_start(out=scale4[:], in_=m_scale.rearrange("a b (g p t) -> p g (a b t)", g=G, t=4))
-        nc.scalar.dma_start(out=gain_raw[:], in_=g.rearrange("(p t) -> p t", t=4))
-        nc.scalar.dma_start(out=bias_raw[:], in_=bm.rearrange("(p t) -> p t", t=4))
+        nc.scalar.dma_start(out=scale4[:], in_=m_scale.rearrange("a b (g p t) -> p g (a b t)", g=PASSES, t=PACK))
+        nc.scalar.dma_start(out=gain_raw[:], in_=g.rearrange("(p t) -> p t", t=PACK))
+        nc.scalar.dma_start(out=bias_raw[:], in_=bm.rearrange("(p t) -> p t", t=PACK))
         nc.sync.dma_start(out=wm_raw[0][:], in_=wm_view[0])
         load_codes(0, 2, 4)
         load_codes(1, 0, 2)
         nc.sync.dma_start(out=wm_raw[1][:], in_=wm_view[1])
         nc.sync.dma_start(out=x_sb[0][:], in_=x_view[0])
         load_codes(1, 2, 4)
-        nc.sync.dma_start(out=w2_raw[:, 0], in_=wg.rearrange("(p j) c -> p j c", j=4))
-        nc.sync.dma_start(out=w2_raw[:, 1], in_=wb.rearrange("(p j) c -> p j c", j=4))
+        nc.sync.dma_start(out=w2_raw[:, 0], in_=wg.rearrange("(p j) c -> p j c", j=PACK))
+        nc.sync.dma_start(out=w2_raw[:, 1], in_=wb.rearrange("(p j) c -> p j c", j=PACK))
         for c in range(2, NCH):
             load_codes(c, 0, 4)
-            if c in (2, 4, 8):
-                b = {2: 1, 4: 2, 8: 3}[c]
-                nc.sync.dma_start(out=x_sb[b][:], in_=x_view[b])
+            for b in X_BEHIND:
+                if X_BEHIND[b] == c:
+                    nc.sync.dma_start(out=x_sb[b][:], in_=x_view[b])
 
         warm = keep.tile([P, 1], F32, name="warm")
         nc.vector.memset(warm[:], 1.0)
@@ -76,28 +81,30 @@ def tile_spademodulationpointwise_t_kernel(tc, x, m_bytes, m_scale, wm, bm, g, w
         nc.vector.tensor_copy(out=ident_b[:], in_=ident_f[:])
         ones = keep.tile([P, 64], BF16, name="ones")
         nc.vector.memset(ones[:], 1.0)
-        sign4 = keep.tile([P, 4], F32, name="sign4")
-        gain4 = keep.tile([P, 4], F32, name="gain4")
-        bias4 = keep.tile([P, 4], F32, name="bias4")
+        sign4 = keep.tile([P, PACK], F32, name="sign4")
+        gain4 = keep.tile([P, PACK], F32, name="gain4")
+        bias4 = keep.tile([P, PACK], F32, name="bias4")
         nc.scalar.activation(out=sign4[:], in_=gain_raw[:], func=ACT.Sign)
         nc.scalar.activation(out=gain4[:], in_=gain_raw[:], func=ACT.Abs)
         nc.vector.tensor_tensor(out=bias4[:], in0=bias_raw[:], in1=gain4[:], op=ALU.mult)
 
-        wm_codes = [keep.tile([P, K], U32, name=f"wm_codes{i}", align_bytes=64) for i in range(G)]
-        wm_scales = [keep.tile([P, K], U8, name=f"wm_scales{i}", align_bytes=64) for i in range(G)]
-        wm_grp = [keep.tile([P, 4 * K], BF16, name=f"wm_grp{i}", align_bytes=64) for i in range(G)]
+        wm_codes = [keep.tile([P, K], U32, name=f"wm_codes{i}", align_bytes=64) for i in range(PASSES)]
+        wm_scales = [keep.tile([P, K], U8, name=f"wm_scales{i}", align_bytes=64) for i in range(PASSES)]
+        wm_grp = [keep.tile([P, PACK * K], BF16, name=f"wm_grp{i}", align_bytes=64) for i in range(PASSES)]
         w2_codes = keep.tile([P, 2 * C], U32, name="w2_codes", align_bytes=64)
         w2_scales = keep.tile([P, 2 * C], U8, name="w2_scales", align_bytes=64)
-        w2_grp = keep.tile([P, 2, C, 4], BF16, name="w2_grp", align_bytes=64)
+        w2_grp = keep.tile([P, 2, C, PACK], BF16, name="w2_grp", align_bytes=64)
 
-        def group_wm(i, eng):
-            src = wm_raw[i][:].rearrange("p (j m t) -> p t m j", j=4, t=4)
-            dst = wm_grp[i][:].rearrange("p (t m j) -> p t m j", t=4, j=4)
-            for t in range(4):
-                if eng == "v":
+        def group_wm(i, on_vector):
+            src = wm_raw[i][:].rearrange("p (j q t) -> p t q j", j=PACK, t=PACK)
+            dst = wm_grp[i][:].rearrange("p (t q j) -> p t q j", t=PACK, j=PACK)
+            for t in range(PACK):
+                if on_vector:
                     nc.vector.tensor_copy(out=dst[:, t], in_=src[:, t])
                 else:
-                    nc.gpsimd.tensor_scalar(out=dst[:, t], in0=src[:, t], scalar1=1.0, scalar2=0.0, op0=ALU.mult, op1=ALU.add)
+                    nc.gpsimd.tensor_scalar(
+                        out=dst[:, t], in0=src[:, t], scalar1=1.0, scalar2=0.0, op0=ALU.mult, op1=ALU.add
+                    )
 
         def quantise_wm(i):
             nc.vector.quantize_mx(out=wm_codes[i][:].bitcast(X4), scales=wm_scales[i][:], in_=wm_grp[i][:])
@@ -106,7 +113,7 @@ def tile_spademodulationpointwise_t_kernel(tc, x, m_bytes, m_scale, wm, bm, g, w
             nc.gpsimd.tensor_tensor(
                 out=w2_grp[:, w],
                 in0=w2_raw[:, w].rearrange("p j c -> p c j"),
-                in1=sign4[:].unsqueeze(1).to_broadcast([P, C, 4]),
+                in1=sign4[:].unsqueeze(1).to_broadcast([P, C, PACK]),
                 op=ALU.mult,
             )
 
@@ -115,110 +122,136 @@ def tile_spademodulationpointwise_t_kernel(tc, x, m_bytes, m_scale, wm, bm, g, w
                 out=w2_codes[:].bitcast(X4), scales=w2_scales[:], in_=w2_grp[:].rearrange("p w c j -> p (w c j)")
             )
 
-        wide, mgrp, mq, hp, apl, agrp, aq, gb, xn, stat, mur, ep = {}, {}, {}, {}, {}, {}, {}, {}, {}, {}, {}, {}
+        wide, banks, m_grp, m_mx, h_bank = {}, {}, {}, {}, {}
+        planes, a_grp, a_mx, maps_bank, products, results = {}, {}, {}, {}, {}, {}
 
         def widen(c, i):
             if i == 0:
                 wide[c] = pool.tile([P, CHUNKS[c][2] * S], BF16, name="wide", align_bytes=64, bufs=3)
             cols = slice(i * S, (i + 1) * S)
+            src = codes_in[c][:, cols].bitcast(FP8)
             if c == 0 and i % 2 == 1:
-                nc.vector.tensor_copy(out=wide[c][:, cols], in_=codes_in[c][:, cols].bitcast(FP8))
+                nc.vector.tensor_copy(out=wide[c][:, cols], in_=src)
             else:
-                nc.scalar.copy(out=wide[c][:, cols], in_=codes_in[c][:, cols].bitcast(FP8))
+                nc.scalar.copy(out=wide[c][:, cols], in_=src)
 
         def turn(c, k):
-            h, gg = divmod(k, G)
+            pair, gg = divmod(k, PASSES)
             words = wide[c][:].bitcast(F32)
-            bank = psum.tile([P, 2, 256], F32, name="turned", bufs=3)
-            for i2 in range(2):
-                i = 2 * h + i2
+            bank = psum.tile([P, 2, 2 * P], F32, name="turned", bufs=3)
+            for i in range(2):
                 for u in range(2):
-                    lo = i * (S // 2) + 256 * gg + u
-                    nc.tensor.transpose(bank[:, u, i2 * P : (i2 + 1) * P], words[:, lo : lo + 255 : 2], ident_f[:])
-            ep[("bank", c, k)] = bank
+                    lo = (2 * pair + i) * (S // 2) + 256 * gg + u
+                    nc.tensor.transpose(bank[:, u, i * P : (i + 1) * P], words[:, lo : lo + 255 : 2], ident_f[:])
+            banks[(c, k)] = bank
 
         def scale_up(c, k):
-            n = CHUNKS[c][2]
-            h, gg = divmod(k, G)
+            pair, gg = divmod(k, PASSES)
             if k == 0:
-                mgrp[c] = pool.tile([P, G, n * P * 4], BF16, name="mgrp", align_bytes=64, bufs=2)
-            bank = ep.pop(("bank", c, k))
+                m_grp[c] = pool.tile([P, PASSES, CHUNKS[c][2] * P * PACK], BF16, name="m_grp", align_bytes=64, bufs=2)
+            bank = banks.pop((c, k))
             src = bank[:].rearrange("p u r -> p (u r)").bitcast(BF16).rearrange("p (u r e) -> p r u e", u=2, e=2)
-            dst = mgrp[c][:, gg, h * 1024 : (h + 1) * 1024].rearrange("p (r u e) -> p r u e", u=2, e=2)
-            sc = scale4[:, gg].rearrange("p (u e) -> p u e", e=2).unsqueeze(1).to_broadcast([P, 256, 2, 2])
+            dst = m_grp[c][:, gg, pair * 1024 : (pair + 1) * 1024].rearrange("p (r u e) -> p r u e", u=2, e=2)
+            sc = scale4[:, gg].rearrange("p (u e) -> p u e", e=2).unsqueeze(1).to_broadcast([P, 2 * P, 2, 2])
             nc.vector.tensor_tensor(out=dst, in0=src, in1=sc, op=ALU.mult)
 
         def quantise_m(c):
             n = CHUNKS[c][2] * P
-            codes = pool.tile([P, G * n], U32, name="m_codes", align_bytes=64, bufs=2)
-            scales = pool.tile([P, G * n], U8, name="m_scales", align_bytes=64, bufs=2)
+            codes = pool.tile([P, PASSES * n], U32, name="m_codes", align_bytes=64, bufs=2)
+            scales = pool.tile([P, PASSES * n], U8, name="m_scales", align_bytes=64, bufs=2)
             nc.vector.quantize_mx(
-                out=codes[:].bitcast(X4), scales=scales[:], in_=mgrp.pop(c)[:].rearrange("p g n -> p (g n)")
+                out=codes[:].bitcast(X4), scales=scales[:], in_=m_grp.pop(c)[:].rearrange("p g n -> p (g n)")
             )
-            mq[c] = (codes, scales)
+            m_mx[c] = (codes, scales)
 
         def embed(c, t):
+            codes, scales = m_mx[c]
             n = CHUNKS[c][2] * P
-            h = psum.tile([P, n], F32, name="embed", bufs=3)
-            for gg in range(G):
-                codes, scales = mq[c]
+            bank = psum.tile([P, n], F32, name="embed", bufs=3)
+            cols = slice(t * P, (t + 1) * P)
+            for gg in range(PASSES):
                 tok = slice(gg * n, (gg + 1) * n)
-                cols = slice(t * P, (t + 1) * P)
                 nc.tensor.matmul_mx(
-                    out=h[:],
+                    out=bank[:],
                     lhsT=wm_codes[gg][:, cols].bitcast(X4),
                     lhsT_scale=wm_scales[gg][:, cols],
                     rhs=codes[:, tok].bitcast(X4),
                     rhs_scale=scales[:, tok],
                     start=(gg == 0),
-                    stop=(gg == G - 1),
+                    stop=(gg == PASSES - 1),
                 )
-            hp[(c, t)] = h
+            h_bank[(c, t)] = bank
 
         def rectify(c, t):
             if t == 0:
-                apl[c] = pool.tile([P, 4, CHUNKS[c][2] * P], BF16, name="apl", align_bytes=64, bufs=2)
+                planes[c] = pool.tile([P, PACK, CHUNKS[c][2] * P], BF16, name="planes", align_bytes=64, bufs=2)
             nc.scalar.activation(
-                out=apl[c][:, t], in_=hp.pop((c, t))[:], func=ACT.Relu, bias=bias4[:, t : t + 1], scale=gain4[:, t : t + 1]
+                out=planes[c][:, t],
+                in_=h_bank.pop((c, t))[:],
+                func=ACT.Relu,
+                bias=bias4[:, t : t + 1],
+                scale=gain4[:, t : t + 1],
             )
 
         def interleave(c):
-            n = CHUNKS[c][2]
-            agrp[c] = pool.tile([P, n * P, 4], BF16, name="agrp", align_bytes=64, bufs=1)
-            src = apl.pop(c)[:].rearrange("p t n -> p n t")
-            if c >= NCH - 3:
-                nc.scalar.copy(out=agrp[c][:], in_=src)
+            a_grp[c] = pool.tile([P, CHUNKS[c][2] * P, PACK], BF16, name="a_grp", align_bytes=64, bufs=1)
+            src = planes.pop(c)[:].rearrange("p t n -> p n t")
+            if c >= SCALAR_INTERLEAVES_FROM:
+                nc.scalar.copy(out=a_grp[c][:], in_=src)
             else:
-                nc.gpsimd.tensor_scalar(out=agrp[c][:], in0=src, scalar1=1.0, scalar2=0.0, op0=ALU.mult, op1=ALU.add)
+                nc.gpsimd.tensor_scalar(out=a_grp[c][:], in0=src, scalar1=1.0, scalar2=0.0, op0=ALU.mult, op1=ALU.add)
 
         def quantise_a(c):
             n = CHUNKS[c][2] * P
             codes = pool.tile([P, n], U32, name="a_codes", align_bytes=64, bufs=2)
             scales = pool.tile([P, n], U8, name="a_scales", align_bytes=64, bufs=2)
             nc.vector.quantize_mx(
-                out=codes[:].bitcast(X4), scales=scales[:], in_=agrp.pop(c)[:].rearrange("p n t -> p (n t)")
+                out=codes[:].bitcast(X4), scales=scales[:], in_=a_grp.pop(c)[:].rearrange("p n t -> p (n t)")
             )
-            aq[c] = (codes, scales)
+            a_mx[c] = (codes, scales)
 
         def maps(c):
-            codes, scales = aq.pop(c)
+            codes, scales = a_mx.pop(c)
             n = CHUNKS[c][2]
-            gam = psum.tile([P, n, C], F32, name="gam", bufs=1)
-            bet = psum.tile([P, n, C], F32, name="bet", bufs=1)
+            gamma = psum.tile([P, n, C], F32, name="gamma", bufs=1)
+            beta = psum.tile([P, n, C], F32, name="beta", bufs=1)
             for i in range(n):
-                cols = slice(i * P, (i + 1) * P)
-                for w, dst in ((0, gam), (1, bet)):
-                    wc = slice(w * C, (w + 1) * C)
+                tok = slice(i * P, (i + 1) * P)
+                for w, bank in ((0, gamma), (1, beta)):
+                    cols = slice(w * C, (w + 1) * C)
                     nc.tensor.matmul_mx(
-                        out=dst[:, i],
-                        lhsT=codes[:, cols].bitcast(X4),
-                        lhsT_scale=scales[:, cols],
-                        rhs=w2_codes[:, wc].bitcast(X4),
-                        rhs_scale=w2_scales[:, wc],
+                        out=bank[:, i],
+                        lhsT=codes[:, tok].bitcast(X4),
+                        lhsT_scale=scales[:, tok],
+                        rhs=w2_codes[:, cols].bitcast(X4),
+                        rhs_scale=w2_scales[:, cols],
                         start=True,
                         stop=True,
                     )
-            gb[c] = (gam, bet)
+            maps_bank[c] = (gamma, beta)
+
+        def modulate1(c):
+            b, r, n = CHUNKS[c]
+            t1 = pool.tile([P, n, C], F32, name="t1")
+            xn = normed[2 * b + r // HALF][:, r % HALF : r % HALF + n]
+            nc.vector.scalar_tensor_tensor(
+                out=t1[:], in0=maps_bank[c][0][:], scalar=1.0, in1=xn, op0=ALU.add, op1=ALU.mult
+            )
+            products[c] = t1
+
+        def modulate2(c):
+            y = pool.tile([P, CHUNKS[c][2], C], F32, name="y")
+            nc.vector.tensor_tensor(out=y[:], in0=maps_bank.pop(c)[1][:], in1=products.pop(c)[:], op=ALU.add)
+            results[c] = y
+
+        def leaky(c):
+            b, r, n = CHUNKS[c]
+            o = pool.tile([P, n, C], F32, name="o", bufs=3)
+            y = results.pop(c)
+            nc.vector.scalar_tensor_tensor(out=o[:], in0=y[:], scalar=0.2, in1=y[:], op0=ALU.mult, op1=ALU.max)
+            nc.sync.dma_start(out=out_view[b][:, r : r + n], in_=o[:])
+
+        stat, spread, normed = {}, {}, {}
 
         def stats_mean(b):
             bank = psum.tile([P, 64], F32, name="turned", bufs=3)
@@ -226,16 +259,16 @@ def tile_spademodulationpointwise_t_kernel(tc, x, m_bytes, m_scale, wm, bm, g, w
                 nc.tensor.matmul(bank[:], lhsT=x_sb[b][:, i], rhs=ones[:], start=(i == 0), stop=(i == ROWS - 1))
             neg_mean = keep.tile([P, 1], F32, name=f"neg_mean{b}")
             nc.scalar.mul(neg_mean[:], bank[:, 0:1], -1.0 / POS)
-            stat[b] = [neg_mean, keep.tile([P, 4], F32, name=f"squares{b}")]
+            stat[b] = (neg_mean, keep.tile([P, 4], F32, name=f"squares{b}"))
 
-        def stats_squares(b, h):
+        def stats_squares(b, q):
             bank = psum.tile([P, 4, P], BF16, name="turned", bufs=3)
             for i in range(4):
-                nc.tensor.transpose(bank[:, i], x_sb[b][:, h * 4 + i], ident_b[:])
-            junk = pool.tile([P, 4, P], BF16, name="junk")
+                nc.tensor.transpose(bank[:, i], x_sb[b][:, q * 4 + i], ident_b[:])
+            squared = pool.tile([P, 4, P], BF16, name="squared")
             neg_mean, squares = stat[b]
             nc.scalar.activation(
-                out=junk[:], in_=bank[:], func=ACT.Square, bias=neg_mean[:], accum_out=squares[:, h : h + 1]
+                out=squared[:], in_=bank[:], func=ACT.Square, bias=neg_mean[:], accum_out=squares[:, q : q + 1]
             )
 
         def stats_sqrt(b):
@@ -243,7 +276,9 @@ def tile_spademodulationpointwise_t_kernel(tc, x, m_bytes, m_scale, wm, bm, g, w
             total = keep.tile([P, 1], F32, name=f"total{b}")
             nc.vector.tensor_reduce(out=total[:], in_=squares[:], axis=mybir.AxisListType.X, op=ALU.add)
             var = keep.tile([P, 1], F32, name=f"var{b}")
-            nc.vector.tensor_scalar(out=var[:], in0=total[:], scalar1=1.0 / POS, scalar2=1e-5, op0=ALU.mult, op1=ALU.add)
+            nc.vector.tensor_scalar(
+                out=var[:], in0=total[:], scalar1=1.0 / POS, scalar2=1e-5, op0=ALU.mult, op1=ALU.add
+            )
             std = keep.tile([P, 1], F32, name=f"std{b}")
             nc.scalar.activation(out=std[:], in_=var[:], func=ACT.Sqrt)
             stat[b] = (neg_mean, std)
@@ -259,106 +294,90 @@ def tile_spademodulationpointwise_t_kernel(tc, x, m_bytes, m_scale, wm, bm, g, w
             bank = psum.tile([P, 2, P], F32, name="turned", bufs=3)
             nc.tensor.matmul(bank[:, 0], lhsT=neg_mean[:].to_broadcast([P, P]), rhs=ident_f[:], start=True, stop=True)
             nc.tensor.matmul(bank[:, 1], lhsT=rstd[:].to_broadcast([P, P]), rhs=ident_f[:], start=True, stop=True)
-            mur[b] = keep.tile([P, 2, C], F32, name=f"mur{b}")
-            nc.scalar.copy(out=mur[b][:], in_=bank[:])
+            spread[b] = keep.tile([P, 2, C], F32, name=f"spread{b}")
+            nc.scalar.copy(out=spread[b][:], in_=bank[:])
 
-        def centre(h):
-            b, r = h // 2, h % 2 * 8
-            xn[h] = pool.tile([P, 8, C], F32, name="xn", bufs=3)
-            nc.gpsimd.tensor_tensor(
-                out=xn[h][:], in0=x_sb[b][:, r : r + 8], in1=mur[b][:, 0:1].to_broadcast([P, 8, C]), op=ALU.add
-            )
+        def centre(half):
+            b, second = divmod(half, 2)
+            rows = slice(second * HALF, (second + 1) * HALF)
+            normed[half] = pool.tile([P, HALF, C], F32, name="normed", bufs=3)
+            mean = spread[b][:, 0:1].to_broadcast([P, HALF, C])
+            nc.gpsimd.tensor_tensor(out=normed[half][:], in0=x_sb[b][:, rows], in1=mean, op=ALU.add)
 
-        def normalise(h):
-            rstd = mur[h // 2][:, 1:2].to_broadcast([P, 8, C])
-            nc.gpsimd.tensor_tensor(out=xn[h][:], in0=xn[h][:], in1=rstd, op=ALU.mult)
+        def normalise(half):
+            rstd = spread[half // 2][:, 1:2].to_broadcast([P, HALF, C])
+            nc.gpsimd.tensor_tensor(out=normed[half][:], in0=normed[half][:], in1=rstd, op=ALU.mult)
 
-        def modulate1(c):
-            b, r, n = CHUNKS[c]
-            t1 = pool.tile([P, n, C], F32, name="t1")
-            rows = xn[2 * b + r // 8][:, r % 8 : r % 8 + n]
-            nc.vector.scalar_tensor_tensor(out=t1[:], in0=gb[c][0][:], scalar=1.0, in1=rows, op0=ALU.add, op1=ALU.mult)
-            ep[("t1", c)] = t1
-
-        def modulate2(c):
-            y = pool.tile([P, CHUNKS[c][2], C], F32, name="y")
-            nc.vector.tensor_tensor(out=y[:], in0=gb.pop(c)[1][:], in1=ep.pop(("t1", c))[:], op=ALU.add)
-            ep[("y", c)] = y
-
-        def leaky(c):
-            b, r, n = CHUNKS[c]
-            o = pool.tile([P, n, C], F32, name="o", bufs=3)
-            y = ep.pop(("y", c))
-            nc.vector.scalar_tensor_tensor(out=o[:], in0=y[:], scalar=0.2, in1=y[:], op0=ALU.mult, op1=ALU.max)
-            nc.sync.dma_start(out=out_view[b][:, r : r + n], in_=o[:])
-
-        def on(f, c, *rest):
+        def on(stage, c, *part):
             if 0 <= c < NCH:
-                if f in (widen, turn, scale_up) and rest[0] >= CHUNKS[c][2]:
+                if stage in (widen, turn, scale_up) and part[0] >= CHUNKS[c][2]:
                     return
-                f(c, *rest)
+                stage(c, *part)
 
         for c in range(2):
             for i in range(4):
                 widen(c, i)
-        group_wm(0, "v")
-        group_wm(1, "g")
+        group_wm(0, True)
+        group_wm(1, False)
         group_w2(0)
         group_w2(1)
+
         for s in range(NCH + 3):
             b, q = divmod(s + 3, 4)
-            done = (s - 1) // 4
-            on(turn, s, 0)
-            on(interleave, s - 2)
-            on(scale_up, s, 0)
+            quarter = 1 <= b < B
+            spreads = q == 0 and b <= B
+            half, second = divmod(s - 1, 2)
             if s:
                 on(widen, s + 1, 0)
-            on(turn, s, 1)
-            on(scale_up, s, 1)
-            if q == 0 and done < B:
-                stats_rstd(done)
-            on(embed, s - 1, 0)
-            on(rectify, s - 1, 0)
+            on(turn, s, 0)
+            on(interleave, s - 2)
             if s:
                 on(widen, s + 1, 1)
+            on(scale_up, s, 0)
+            if spreads:
+                stats_rstd(b - 1)
+            on(turn, s, 1)
+            on(embed, s - 1, 0)
             on(maps, s - 3)
+            if spreads:
+                stats_spread(b - 1)
             on(modulate1, s - 3)
             on(turn, s, 2)
-            if q == 0 and done < B:
-                stats_spread(done)
-            on(scale_up, s, 2)
-            if 1 <= b < B and q == 0:
-                stats_mean(b)
-            on(embed, s - 1, 1)
-            on(rectify, s - 1, 1)
-            if s:
-                on(widen, s + 1, 2)
-            on(modulate2, s - 3)
-            if 1 <= b < B:
-                stats_squares(b, q)
             on(turn, s, 3)
-            on(scale_up, s, 3)
             if s == 0:
                 stats_mean(0)
                 for i in range(4):
                     stats_squares(0, i)
-            on(embed, s - 1, 2)
-            on(rectify, s - 1, 2)
+            on(scale_up, s, 1)
+            on(scale_up, s, 2)
             if s:
-                on(widen, s + 1, 3)
+                on(widen, s + 1, 2)
+            if 0 <= half < 2 * B:
+                (normalise if second else centre)(half)
+            on(rectify, s - 1, 0)
+            on(embed, s - 1, 1)
+            on(scale_up, s, 3)
+            on(rectify, s - 1, 1)
+            on(embed, s - 1, 2)
+            on(modulate2, s - 3)
+            on(quantise_m, s)
+            if quarter and q == 0:
+                stats_mean(b)
+            on(embed, s - 1, 3)
+            on(quantise_a, s - 2)
+            on(rectify, s - 1, 2)
+            on(rectify, s - 1, 3)
             if s == 0:
                 quantise_wm(0)
                 quantise_wm(1)
-            if s == 2:
-                quantise_w2()
-            on(embed, s - 1, 3)
-            on(rectify, s - 1, 3)
-            on(leaky, s - 3)
-            on(quantise_m, s)
-            on(quantise_a, s - 2)
+            if quarter:
+                stats_squares(b, q)
             if s == 0:
                 stats_sqrt(0)
-            if 1 <= b < B and q == 3:
+            on(leaky, s - 3)
+            if s:
+                on(widen, s + 1, 3)
+            if s == 2:
+                quantise_w2()
+            if quarter and q == 3:
                 stats_sqrt(b)
-            if 0 < s < 17:
-                (centre if s % 2 else normalise)((s - 1) // 2)

from contextlib import ExitStack

import concourse.mybir as mybir
from concourse.masks import make_identity

B, POS, S, K, C = 4, 2048, 1024, 512, 128
FLOPS = 2 * B * POS * (S * K + 2 * K * C)

F32 = mybir.dt.float32
BF16 = mybir.dt.bfloat16
U32 = mybir.dt.uint32
U8 = mybir.dt.uint8
FP8 = mybir.dt.float8_e4m3fn
X4 = mybir.dt.float8_e4m3fn_x4
ALU = mybir.AluOpType
ACT = mybir.ActivationFunctionType

P = 128
PACK = 4
PASSES = S // (P * PACK)
ROWS = POS // P
HALF = ROWS // 2

CHUNKS = [(b, r, 4) for b in range(B) for r in range(0, ROWS, 4)][:-1] + [(B - 1, 12, 2), (B - 1, 14, 2)]
NCH = len(CHUNKS)
SCALAR_INTERLEAVES_FROM = NCH - 3
X_BEHIND = {1: 2, 2: 4, 3: 8}


def tile_spademodulationpointwise_t_kernel(tc, x, m_bytes, m_scale, wm, bm, g, wg, wb, out):
    nc = tc.nc
    with ExitStack() as ctx:
        keep = ctx.enter_context(tc.tile_pool(name="keep", bufs=1))
        pool = ctx.enter_context(tc.tile_pool(name="pool", bufs=2))
        psum = ctx.enter_context(tc.psum_pool(name="psum", bufs=1))
        ctx.enter_context(tc.manual_schedule())

        m_view = m_bytes.rearrange("b (p i) k -> b p (i k)", i=ROWS)
        x_view = x.rearrange("b (p i) c -> b p i c", i=ROWS)
        out_view = out.rearrange("b (p i) c -> b p i c", i=ROWS)
        wm_view = wm.rearrange("(g p j) c -> g p (j c)", p=P, j=PACK)

        codes_in = [keep.tile([P, CHUNKS[c][2] * S], U8, name=f"codes_in{c}", align_bytes=64) for c in range(NCH)]
        x_sb = [keep.tile([P, ROWS, C], BF16, name=f"x_sb{b}", align_bytes=64) for b in range(B)]
        wm_raw = [keep.tile([P, PACK * K], BF16, name=f"wm_raw{i}", align_bytes=64) for i in range(PASSES)]
        w2_raw = keep.tile([P, 2, PACK, C], BF16, name="w2_raw", align_bytes=64)
        scale4 = keep.tile([P, PASSES, PACK], F32, name="scale4")
        gain_raw = keep.tile([P, PACK], BF16, name="gain_raw")
        bias_raw = keep.tile([P, PACK], BF16, name="bias_raw")

        def load_codes(c, i0, i1):
            b, r, n = CHUNKS[c]
            i1 = min(i1, n)
            nc.sync.dma_start(out=codes_in[c][:, i0 * S : i1 * S], in_=m_view[b][:, (r + i0) * S : (r + i1) * S])

        load_codes(0, 0, 1)
        load_codes(0, 1, 2)
        nc.scalar.dma_start(out=scale4[:], in_=m_scale.rearrange("a b (g p t) -> p g (a b t)", g=PASSES, t=PACK))
        nc.scalar.dma_start(out=gain_raw[:], in_=g.rearrange("(p t) -> p t", t=PACK))
        nc.scalar.dma_start(out=bias_raw[:], in_=bm.rearrange("(p t) -> p t", t=PACK))
        nc.sync.dma_start(out=wm_raw[0][:], in_=wm_view[0])
        load_codes(0, 2, 4)
        load_codes(1, 0, 2)
        nc.sync.dma_start(out=wm_raw[1][:], in_=wm_view[1])
        nc.sync.dma_start(out=x_sb[0][:], in_=x_view[0])
        load_codes(1, 2, 4)
        nc.sync.dma_start(out=w2_raw[:, 0], in_=wg.rearrange("(p j) c -> p j c", j=PACK))
        nc.sync.dma_start(out=w2_raw[:, 1], in_=wb.rearrange("(p j) c -> p j c", j=PACK))
        for c in range(2, NCH):
            load_codes(c, 0, 4)
            for b in X_BEHIND:
                if X_BEHIND[b] == c:
                    nc.sync.dma_start(out=x_sb[b][:], in_=x_view[b])

        warm = keep.tile([P, 1], F32, name="warm")
        nc.vector.memset(warm[:], 1.0)
        nc.scalar.activation(out=warm[:], in_=warm[:], func=ACT.Sqrt)
        ident_f = keep.tile([P, P], F32, name="ident_f")
        make_identity(nc, ident_f[:])
        ident_b = keep.tile([P, P], BF16, name="ident_b")
        nc.vector.tensor_copy(out=ident_b[:], in_=ident_f[:])
        ones = keep.tile([P, 64], BF16, name="ones")
        nc.vector.memset(ones[:], 1.0)
        sign4 = keep.tile([P, PACK], F32, name="sign4")
        gain4 = keep.tile([P, PACK], F32, name="gain4")
        bias4 = keep.tile([P, PACK], F32, name="bias4")
        nc.scalar.activation(out=sign4[:], in_=gain_raw[:], func=ACT.Sign)
        nc.scalar.activation(out=gain4[:], in_=gain_raw[:], func=ACT.Abs)
        nc.vector.tensor_tensor(out=bias4[:], in0=bias_raw[:], in1=gain4[:], op=ALU.mult)

        wm_codes = [keep.tile([P, K], U32, name=f"wm_codes{i}", align_bytes=64) for i in range(PASSES)]
        wm_scales = [keep.tile([P, K], U8, name=f"wm_scales{i}", align_bytes=64) for i in range(PASSES)]
        wm_grp = [keep.tile([P, PACK * K], BF16, name=f"wm_grp{i}", align_bytes=64) for i in range(PASSES)]
        w2_codes = keep.tile([P, 2 * C], U32, name="w2_codes", align_bytes=64)
        w2_scales = keep.tile([P, 2 * C], U8, name="w2_scales", align_bytes=64)
        w2_grp = keep.tile([P, 2, C, PACK], BF16, name="w2_grp", align_bytes=64)

        def group_wm(i, on_vector):
            src = wm_raw[i][:].rearrange("p (j q t) -> p t q j", j=PACK, t=PACK)
            dst = wm_grp[i][:].rearrange("p (t q j) -> p t q j", t=PACK, j=PACK)
            for t in range(PACK):
                if on_vector:
                    nc.vector.tensor_copy(out=dst[:, t], in_=src[:, t])
                else:
                    nc.gpsimd.tensor_scalar(
                        out=dst[:, t], in0=src[:, t], scalar1=1.0, scalar2=0.0, op0=ALU.mult, op1=ALU.add
                    )

        def quantise_wm(i):
            nc.vector.quantize_mx(out=wm_codes[i][:].bitcast(X4), scales=wm_scales[i][:], in_=wm_grp[i][:])

        def group_w2(w):
            nc.gpsimd.tensor_tensor(
                out=w2_grp[:, w],
                in0=w2_raw[:, w].rearrange("p j c -> p c j"),
                in1=sign4[:].unsqueeze(1).to_broadcast([P, C, PACK]),
                op=ALU.mult,
            )

        def quantise_w2():
            nc.vector.quantize_mx(
                out=w2_codes[:].bitcast(X4), scales=w2_scales[:], in_=w2_grp[:].rearrange("p w c j -> p (w c j)")
            )

        wide, banks, m_grp, m_mx, h_bank = {}, {}, {}, {}, {}
        planes, a_grp, a_mx, maps_bank, products, results = {}, {}, {}, {}, {}, {}

        def widen(c, i):
            if i == 0:
                wide[c] = pool.tile([P, CHUNKS[c][2] * S], BF16, name="wide", align_bytes=64, bufs=3)
            cols = slice(i * S, (i + 1) * S)
            src = codes_in[c][:, cols].bitcast(FP8)
            if c == 0 and i % 2 == 1:
                nc.vector.tensor_copy(out=wide[c][:, cols], in_=src)
            else:
                nc.scalar.copy(out=wide[c][:, cols], in_=src)

        def turn(c, k):
            pair, gg = divmod(k, PASSES)
            words = wide[c][:].bitcast(F32)
            bank = psum.tile([P, 2, 2 * P], F32, name="turned", bufs=3)
            for i in range(2):
                for u in range(2):
                    lo = (2 * pair + i) * (S // 2) + 256 * gg + u
                    nc.tensor.transpose(bank[:, u, i * P : (i + 1) * P], words[:, lo : lo + 255 : 2], ident_f[:])
            banks[(c, k)] = bank

        def scale_up(c, k):
            pair, gg = divmod(k, PASSES)
            if k == 0:
                m_grp[c] = pool.tile([P, PASSES, CHUNKS[c][2] * P * PACK], BF16, name="m_grp", align_bytes=64, bufs=2)
            bank = banks.pop((c, k))
            src = bank[:].rearrange("p u r -> p (u r)").bitcast(BF16).rearrange("p (u r e) -> p r u e", u=2, e=2)
            dst = m_grp[c][:, gg, pair * 1024 : (pair + 1) * 1024].rearrange("p (r u e) -> p r u e", u=2, e=2)
            sc = scale4[:, gg].rearrange("p (u e) -> p u e", e=2).unsqueeze(1).to_broadcast([P, 2 * P, 2, 2])
            nc.vector.tensor_tensor(out=dst, in0=src, in1=sc, op=ALU.mult)

        def quantise_m(c):
            n = CHUNKS[c][2] * P
            codes = pool.tile([P, PASSES * n], U32, name="m_codes", align_bytes=64, bufs=2)
            scales = pool.tile([P, PASSES * n], U8, name="m_scales", align_bytes=64, bufs=2)
            nc.vector.quantize_mx(
                out=codes[:].bitcast(X4), scales=scales[:], in_=m_grp.pop(c)[:].rearrange("p g n -> p (g n)")
            )
            m_mx[c] = (codes, scales)

        def embed(c, t):
            codes, scales = m_mx[c]
            n = CHUNKS[c][2] * P
            bank = psum.tile([P, n], F32, name="embed", bufs=3)
            cols = slice(t * P, (t + 1) * P)
            for gg in range(PASSES):
                tok = slice(gg * n, (gg + 1) * n)
                nc.tensor.matmul_mx(
                    out=bank[:],
                    lhsT=wm_codes[gg][:, cols].bitcast(X4),
                    lhsT_scale=wm_scales[gg][:, cols],
                    rhs=codes[:, tok].bitcast(X4),
                    rhs_scale=scales[:, tok],
                    start=(gg == 0),
                    stop=(gg == PASSES - 1),
                )
            h_bank[(c, t)] = bank

        def rectify(c, t):
            if t == 0:
                planes[c] = pool.tile([P, PACK, CHUNKS[c][2] * P], BF16, name="planes", align_bytes=64, bufs=2)
            nc.scalar.activation(
                out=planes[c][:, t],
                in_=h_bank.pop((c, t))[:],
                func=ACT.Relu,
                bias=bias4[:, t : t + 1],
                scale=gain4[:, t : t + 1],
            )

        def interleave(c):
            a_grp[c] = pool.tile([P, CHUNKS[c][2] * P, PACK], BF16, name="a_grp", align_bytes=64, bufs=1)
            src = planes.pop(c)[:].rearrange("p t n -> p n t")
            if c >= SCALAR_INTERLEAVES_FROM:
                nc.scalar.copy(out=a_grp[c][:], in_=src)
            else:
                nc.gpsimd.tensor_scalar(out=a_grp[c][:], in0=src, scalar1=1.0, scalar2=0.0, op0=ALU.mult, op1=ALU.add)

        def quantise_a(c):
            n = CHUNKS[c][2] * P
            codes = pool.tile([P, n], U32, name="a_codes", align_bytes=64, bufs=2)
            scales = pool.tile([P, n], U8, name="a_scales", align_bytes=64, bufs=2)
            nc.vector.quantize_mx(
                out=codes[:].bitcast(X4), scales=scales[:], in_=a_grp.pop(c)[:].rearrange("p n t -> p (n t)")
            )
            a_mx[c] = (codes, scales)

        def maps(c):
            codes, scales = a_mx.pop(c)
            n = CHUNKS[c][2]
            gamma = psum.tile([P, n, C], F32, name="gamma", bufs=1)
            beta = psum.tile([P, n, C], F32, name="beta", bufs=1)
            for i in range(n):
                tok = slice(i * P, (i + 1) * P)
                for w, bank in ((0, gamma), (1, beta)):
                    cols = slice(w * C, (w + 1) * C)
                    nc.tensor.matmul_mx(
                        out=bank[:, i],
                        lhsT=codes[:, tok].bitcast(X4),
                        lhsT_scale=scales[:, tok],
                        rhs=w2_codes[:, cols].bitcast(X4),
                        rhs_scale=w2_scales[:, cols],
                        start=True,
                        stop=True,
                    )
            maps_bank[c] = (gamma, beta)

        def modulate1(c):
            b, r, n = CHUNKS[c]
            t1 = pool.tile([P, n, C], F32, name="t1")
            xn = normed[2 * b + r // HALF][:, r % HALF : r % HALF + n]
            nc.vector.scalar_tensor_tensor(
                out=t1[:], in0=maps_bank[c][0][:], scalar=1.0, in1=xn, op0=ALU.add, op1=ALU.mult
            )
            products[c] = t1

        def modulate2(c):
            y = pool.tile([P, CHUNKS[c][2], C], F32, name="y")
            nc.vector.tensor_tensor(out=y[:], in0=maps_bank.pop(c)[1][:], in1=products.pop(c)[:], op=ALU.add)
            results[c] = y

        def leaky(c):
            b, r, n = CHUNKS[c]
            o = pool.tile([P, n, C], F32, name="o", bufs=3)
            y = results.pop(c)
            nc.vector.scalar_tensor_tensor(out=o[:], in0=y[:], scalar=0.2, in1=y[:], op0=ALU.mult, op1=ALU.max)
            nc.sync.dma_start(out=out_view[b][:, r : r + n], in_=o[:])

        stat, spread, normed = {}, {}, {}

        def stats_mean(b):
            bank = psum.tile([P, 64], F32, name="turned", bufs=3)
            for i in range(ROWS):
                nc.tensor.matmul(bank[:], lhsT=x_sb[b][:, i], rhs=ones[:], start=(i == 0), stop=(i == ROWS - 1))
            neg_mean = keep.tile([P, 1], F32, name=f"neg_mean{b}")
            nc.scalar.mul(neg_mean[:], bank[:, 0:1], -1.0 / POS)
            stat[b] = (neg_mean, keep.tile([P, 4], F32, name=f"squares{b}"))

        def stats_squares(b, q):
            bank = psum.tile([P, 4, P], BF16, name="turned", bufs=3)
            for i in range(4):
                nc.tensor.transpose(bank[:, i], x_sb[b][:, q * 4 + i], ident_b[:])
            squared = pool.tile([P, 4, P], BF16, name="squared")
            neg_mean, squares = stat[b]
            nc.scalar.activation(
                out=squared[:], in_=bank[:], func=ACT.Square, bias=neg_mean[:], accum_out=squares[:, q : q + 1]
            )

        def stats_sqrt(b):
            neg_mean, squares = stat[b]
            total = keep.tile([P, 1], F32, name=f"total{b}")
            nc.vector.tensor_reduce(out=total[:], in_=squares[:], axis=mybir.AxisListType.X, op=ALU.add)
            var = keep.tile([P, 1], F32, name=f"var{b}")
            nc.vector.tensor_scalar(
                out=var[:], in0=total[:], scalar1=1.0 / POS, scalar2=1e-5, op0=ALU.mult, op1=ALU.add
            )
            std = keep.tile([P, 1], F32, name=f"std{b}")
            nc.scalar.activation(out=std[:], in_=var[:], func=ACT.Sqrt)
            stat[b] = (neg_mean, std)

        def stats_rstd(b):
            neg_mean, std = stat[b]
            rstd = keep.tile([P, 1], F32, name=f"rstd{b}")
            nc.vector.reciprocal(out=rstd[:], in_=std[:])
            stat[b] = (neg_mean, rstd)

        def stats_spread(b):
            neg_mean, rstd = stat[b]
            bank = psum.tile([P, 2, P], F32, name="turned", bufs=3)
            nc.tensor.matmul(bank[:, 0], lhsT=neg_mean[:].to_broadcast([P, P]), rhs=ident_f[:], start=True, stop=True)
            nc.tensor.matmul(bank[:, 1], lhsT=rstd[:].to_broadcast([P, P]), rhs=ident_f[:], start=True, stop=True)
            spread[b] = keep.tile([P, 2, C], F32, name=f"spread{b}")
            nc.scalar.copy(out=spread[b][:], in_=bank[:])

        def centre(half):
            b, second = divmod(half, 2)
            rows = slice(second * HALF, (second + 1) * HALF)
            normed[half] = pool.tile([P, HALF, C], F32, name="normed", bufs=3)
            mean = spread[b][:, 0:1].to_broadcast([P, HALF, C])
            nc.gpsimd.tensor_tensor(out=normed[half][:], in0=x_sb[b][:, rows], in1=mean, op=ALU.add)

        def normalise(half):
            rstd = spread[half // 2][:, 1:2].to_broadcast([P, HALF, C])
            nc.gpsimd.tensor_tensor(out=normed[half][:], in0=normed[half][:], in1=rstd, op=ALU.mult)

        def on(stage, c, *part):
            if 0 <= c < NCH:
                if stage in (widen, turn, scale_up) and part[0] >= CHUNKS[c][2]:
                    return
                stage(c, *part)

        for c in range(2):
            for i in range(4):
                widen(c, i)
        group_wm(0, True)
        group_wm(1, False)
        group_w2(0)
        group_w2(1)

        for s in range(NCH + 3):
            b, q = divmod(s + 3, 4)
            quarter = 1 <= b < B
            spreads = q == 0 and b <= B
            half, second = divmod(s - 1, 2)
            if s:
                on(widen, s + 1, 0)
            on(turn, s, 0)
            on(interleave, s - 2)
            if s:
                on(widen, s + 1, 1)
            on(scale_up, s, 0)
            if spreads:
                stats_rstd(b - 1)
            on(turn, s, 1)
            on(embed, s - 1, 0)
            on(maps, s - 3)
            if spreads:
                stats_spread(b - 1)
            on(modulate1, s - 3)
            on(turn, s, 2)
            on(turn, s, 3)
            if s == 0:
                stats_mean(0)
                for i in range(4):
                    stats_squares(0, i)
            on(scale_up, s, 1)
            on(scale_up, s, 2)
            if s:
                on(widen, s + 1, 2)
            if 0 <= half < 2 * B:
                (normalise if second else centre)(half)
            on(rectify, s - 1, 0)
            on(embed, s - 1, 1)
            on(scale_up, s, 3)
            on(rectify, s - 1, 1)
            on(embed, s - 1, 2)
            on(modulate2, s - 3)
            on(quantise_m, s)
            if quarter and q == 0:
                stats_mean(b)
            on(embed, s - 1, 3)
            on(quantise_a, s - 2)
            on(rectify, s - 1, 2)
            on(rectify, s - 1, 3)
            if s == 0:
                quantise_wm(0)
                quantise_wm(1)
            if quarter:
                stats_squares(b, q)
            if s == 0:
                stats_sqrt(0)
            on(leaky, s - 3)
            if s:
                on(widen, s + 1, 3)
            if s == 2:
                quantise_w2()
            if quarter and q == 3:
                stats_sqrt(b)
